import numpy as np
import ml_dtypes


def mxq(x, axis, fmt="e4m3"):
    dtype, down = {"e4m3": (ml_dtypes.float8_e4m3fn, 7), "e5m2": (ml_dtypes.float8_e5m2, 14)}[fmt]
    v = np.moveaxis(np.asarray(x, np.float32).astype(ml_dtypes.bfloat16).astype(np.float64), axis, -1)
    blocks = v.reshape(v.shape[:-1] + (-1, 32))
    amax = np.abs(blocks).max(-1, keepdims=True)
    byte = np.maximum(np.where(amax > 0, np.frexp(amax)[1] - 1 + 127, 0) - down, 1)
    scale = np.exp2(byte - 127.0)
    codes = (blocks / scale).astype(np.float32).astype(dtype).astype(np.float64)
    return np.moveaxis((codes * scale).reshape(v.shape), -1, axis)


WIDE = False


def mx_kscale(k):
    if not WIDE:
        return np.ones(k)
    levels = np.array([10, -10, 5, -5, 0])
    if k % 512:
        return np.exp2(np.random.permutation(np.resize(levels, k // 32))).repeat(32)
    a = np.empty((k // 512, 16))
    for p in range(k // 512):
        a[p, :8] = np.random.permutation(np.resize(levels, 8))
        for g in range(8):
            far = levels[np.abs(levels - a[p, g]) >= 10]
            a[p, g + 8] = far[np.random.randint(len(far))]
    return np.exp2(a.ravel()).repeat(32)


BF16 = ml_dtypes.bfloat16


def bf(x):
    return np.asarray(x, np.float32).astype(BF16)


def f64(x):
    return np.asarray(x).astype(np.float64)

def planes(Y):
    n, m = Y.shape
    b = f64(bf(Y)).reshape(n // 32, 32, m)
    amax = np.abs(b).max(1)
    byte = np.clip(np.where(amax > 0, np.frexp(amax)[1] - 1 + 127 - 7, 1), 1, 254)
    codes = (b * np.exp2(127.0 - byte)[:, None, :]).reshape(n, m).astype(np.float32).astype(ml_dtypes.float8_e4m3fn).view(np.uint8)
    words = codes.reshape(n // 512, 128, 4, m).transpose(0, 1, 3, 2)
    return np.ascontiguousarray(words), np.ascontiguousarray(byte.astype(np.uint8).reshape(n // 512, 16, m))


B, S, Z, E = 2, 1024, 512, 1024


def sigmoid(x):
    return 1.0 / (1.0 + np.exp(-x))


def squared_relu(t):
    r = np.maximum(t, 0.0)
    return r * r


def setup_inputs():
    s = mx_kscale(Z)
    r = mx_kscale(S)
    return {
        "z": bf(np.random.standard_normal((B, S, Z))),
        "gq": bf(np.random.standard_normal(Z) * s),
        "cq": bf(0.5 * np.random.standard_normal(Z) * s),
        "gk": bf(np.random.standard_normal(Z) / s),
        "g": bf(np.random.standard_normal(S) * r),
        "v": bf(0.25 * np.random.standard_normal((B, S, E)) / r[None, :, None]),
        "u": bf(np.random.standard_normal((B, S, E))),
    }


def core(z, gq, cq, gk, g, v, u):
    z, gq, cq, gk, g, v, u = f64(z), f64(gq), f64(cq), f64(gk), f64(g), f64(v), f64(u)
    width = z.shape[-1]
    q = z * gq[None, None, :] + cq[None, None, :]
    k = z * gk[None, None, :]
    t = (mxq(q, 2, "e4m3") @ mxq(k, 2, "e4m3").transpose(0, 2, 1)) / np.sqrt(width)
    a = squared_relu(t) / 8.0
    p = a * g[None, None, :]
    c = mxq(p, 2, "e4m3") @ mxq(v, 1, "e4m3")
    return u * sigmoid(u) * c


def reference(z, gq, cq, gk, g, v, u):
    R_out = core(z, gq, cq, gk, g, v, u)
    words, scales = planes(np.moveaxis(R_out, 2, 0).reshape(1024, -1))
    return R_out, words, scales

@@ -1,0 +1,373 @@
+from contextlib import ExitStack
+
+import concourse.mybir as mybir
+from concourse.masks import make_identity
+
+B, S, Z, E = 2, 1024, 512, 1024
+P = 128
+FLOPS = 2 * B * S * S * (Z + E)
+
+F32 = mybir.dt.float32
+BF16 = mybir.dt.bfloat16
+U32 = mybir.dt.uint32
+I32 = mybir.dt.int32
+U8 = mybir.dt.uint8
+FP8X4 = mybir.dt.float8_e4m3fn_x4
+ACT = mybir.ActivationFunctionType
+ALU = mybir.AluOpType
+
+
+def tile_gatedattentionunitsquaredrelu_x1_kernel(tc, z, gq, cq, gk, g, v, u, out_0, out_1, out_2):
+    nc = tc.nc
+    with ExitStack() as ctx:
+        const = ctx.enter_context(tc.tile_pool(name="const", bufs=1))
+        work = ctx.enter_context(tc.tile_pool(name="work", bufs=2))
+        ps = ctx.enter_context(tc.psum_pool(name="ps", bufs=2))
+
+        gq_raw = const.tile([P, 4], BF16, name="gq_raw")
+        cq_raw = const.tile([P, 4], BF16, name="cq_raw")
+        gk_raw = const.tile([P, 4], BF16, name="gk_raw")
+        g_raw = const.tile([P, 2, 4], BF16, name="g_raw")
+        nc.scalar.dma_start(out=gk_raw[:], in_=gk.rearrange("(p t) -> p t", t=4))
+        nc.scalar.dma_start(out=gq_raw[:], in_=gq.rearrange("(p t) -> p t", t=4))
+        nc.scalar.dma_start(out=cq_raw[:], in_=cq.rearrange("(p t) -> p t", t=4))
+        nc.scalar.dma_start(out=g_raw[:], in_=g.rearrange("(h p t) -> p h t", h=2, t=4))
+
+        z_sb, v_sb, u_sb = {}, {}, {}
+
+        def load_z(b, h, parts):
+            z_sb[b, h] = const.tile([P, 4, Z], BF16, name="z%d%d" % (b, h))
+            src = z[b, h * 512 : (h + 1) * 512, :].rearrange("(m t) c -> m t c", t=4)
+            w = 4 // parts
+            for i in range(parts):
+                nc.sync.dma_start(out=z_sb[b, h][:, i * w : (i + 1) * w, :], in_=src[:, i * w : (i + 1) * w, :])
+
+        def load_rows(store, src, name, b, h):
+            store[b, h] = const.tile([P, 4, E], BF16, name="%s%d%d" % (name, b, h))
+            nc.sync.dma_start(out=store[b, h][:], in_=src[b, h * 512 : (h + 1) * 512, :].rearrange("(m t) e -> m t e", t=4))
+
+        load_z(0, 0, 2)
+        load_z(0, 1, 2)
+        load_rows(v_sb, v, "v", 0, 0)
+        load_rows(v_sb, v, "v", 0, 1)
+        load_rows(u_sb, u, "u", 0, 0)
+        load_z(1, 0, 1)
+        load_z(1, 1, 1)
+        load_rows(u_sb, u, "u", 0, 1)
+        load_rows(v_sb, v, "v", 1, 0)
+        load_rows(v_sb, v, "v", 1, 1)
+        load_rows(u_sb, u, "u", 1, 0)
+        load_rows(u_sb, u, "u", 1, 1)
+
+        warm = const.tile([P, 1], F32, name="warm")
+        nc.vector.memset(warm[:], 0.0)
+        warm2 = const.tile([P, 1], F32, name="warm2")
+        nc.scalar.activation(out=warm2[:], in_=warm[:], func=ACT.Silu)
+        ident = const.tile([P, P], F32, name="ident")
+        make_identity(nc, ident[:])
+        identb = const.tile([P, P], BF16, name="identb")
+        make_identity(nc, identb[:])
+        gq32 = const.tile([P, 4], F32, name="gq32")
+        cq32 = const.tile([P, 4], F32, name="cq32")
+        gs = const.tile([P, 8], F32, name="gs")
+        nc.vector.tensor_copy(out=gq32[:], in_=gq_raw[:])
+        nc.vector.tensor_copy(out=cq32[:], in_=cq_raw[:])
+        nc.vector.tensor_scalar(out=gs[:], in0=g_raw[:].rearrange("p h t -> p (h t)"), scalar1=1.0 / 4096.0, scalar2=None, op0=ALU.mult)
+
+        kc, ks, qc, qs, vc, vs = {}, {}, {}, {}, {}, {}
+        for b in range(B):
+            kc[b] = const.tile([P, S], U32, name="kc%d" % b, align_bytes=64)
+            ks[b] = const.tile([P, S], U8, name="ks%d" % b, align_bytes=64)
+            qc[b] = const.tile([P, S], U32, name="qc%d" % b, align_bytes=64)
+            qs[b] = const.tile([P, S], U8, name="qs%d" % b, align_bytes=64)
+            for h in range(2):
+                vc[b, h] = const.tile([P, E], U32, name="vc%d%d" % (b, h), align_bytes=64)
+                vs[b, h] = const.tile([P, E], U8, name="vs%d%d" % (b, h), align_bytes=64)
+
+        kb, qp, qb = {}, {}, {}
+
+        def z_task(b, zb):
+            h, tp = divmod(zb, 2)
+            bank = ps.tile([P, 2, 2, P], F32, name="tr", bufs=3)
+            words = z_sb[b, h][:].rearrange("p t c -> p (t c)").bitcast(F32)
+            for a in range(2):
+                t = 2 * tp + a
+                for w in range(2):
+                    nc.tensor.transpose(bank[:, w, a, :], words[:, 256 * t + w : 256 * (t + 1) : 2], ident[:])
+            zv = bank[:].rearrange("p w a m -> p (w a m)").bitcast(BF16).rearrange("p (w i e) -> p w i e", w=2, e=2)
+            kt = work.tile([P, 1024], BF16, name="kb", bufs=3, align_bytes=64)
+            kb[b, zb] = kt
+            nc.vector.tensor_tensor(
+                out=kt[:].rearrange("p (i w e) -> p i w e", w=2, e=2),
+                in0=zv.rearrange("p w i e -> p i w e"),
+                in1=gk_raw[:].rearrange("p (w e) -> p w e", e=2).unsqueeze(1).to_broadcast([P, 256, 2, 2]),
+                op=ALU.mult,
+            )
+            qt = work.tile([P, 32, 4, 8], BF16, name="qp", bufs=2)
+            qp[b, zb] = qt
+            for t in range(4):
+                w, e = divmod(t, 2)
+                nc.scalar.activation(
+                    out=qt[:, :, t, :],
+                    in_=zv[:, w, :, e].rearrange("p (c i) -> p c i", i=8),
+                    func=ACT.Identity,
+                    scale=gq32[:, t : t + 1],
+                    bias=cq32[:, t : t + 1],
+                )
+
+        def quant_k(b, zb):
+            cols = slice(zb * 256, (zb + 1) * 256)
+            nc.vector.quantize_mx(out=kc[b][:, cols].bitcast(FP8X4), scales=ks[b][:, cols], in_=kb[b, zb][:])
+
+        def interleave_q(b, zb):
+            qt = work.tile([P, 1024], BF16, name="qb", bufs=3, align_bytes=64)
+            qb[b, zb] = qt
+            nc.vector.tensor_copy(
+                out=qt[:].rearrange("p (c i t) -> p c i t", i=8, t=4), in_=qp[b, zb][:].rearrange("p c t i -> p c i t")
+            )
+
+        def quant_q(b, zb):
+            cols = slice(zb * 256, (zb + 1) * 256)
+            nc.vector.quantize_mx(out=qc[b][:, cols].bitcast(FP8X4), scales=qs[b][:, cols], in_=qb[b, zb][:])
+
+        vb = {}
+
+        def v_task(b, h, e4, engine):
+            bank = ps.tile([P, 4, 256], BF16, name="tr", bufs=3)
+            for t in range(4):
+                nc.tensor.matmul(bank[:, t, :], lhsT=identb[:], rhs=v_sb[b, h][:, t, e4 * 256 : (e4 + 1) * 256], start=True, stop=True)
+            if e4 % 2 == 0:
+                vt = work.tile([P, 2, 1024], BF16, name="vb", bufs=2, align_bytes=64)
+                vb[b, h, e4 // 2] = vt
+            dst = vb[b, h, e4 // 2][:, e4 % 2, :].rearrange("p (i t) -> p i t", t=4)
+            src = bank[:].rearrange("p t i -> p i t")
+            if engine == "s":
+                nc.scalar.copy(out=dst, in_=src)
+            else:
+                nc.vector.tensor_copy(out=dst, in_=src)
+
+        def quant_v(b, h, e2):
+            cols = slice(e2 * 512, (e2 + 1) * 512)
+            nc.vector.quantize_mx(
+                out=vc[b, h][:, cols].bitcast(FP8X4), scales=vs[b, h][:, cols], in_=vb[b, h, e2][:].rearrange("p a x -> p (a x)")
+            )
+
+        def where(n):
+            b, r = divmod(n, 8)
+            h, t = divmod(r, 4)
+            return b, h, t, slice(r * P, (r + 1) * P)
+
+        st, tg, pb, pc, psc, cb, gate, o32, ob, gr, oc, osc = {}, {}, {}, {}, {}, {}, {}, {}, {}, {}, {}, {}
+
+        def st1(n, hh):
+            b, h, t, cols = where(n)
+            bank = ps.tile([P, 4, P], F32, name="st", bufs=3)
+            st[n, hh] = bank
+            for tk in range(4):
+                kcols = slice(hh * 512 + tk * P, hh * 512 + (tk + 1) * P)
+                nc.tensor.matmul_mx(
+                    out=bank[:, tk, :],
+                    lhsT=kc[b][:, kcols].bitcast(FP8X4),
+                    lhsT_scale=ks[b][:, kcols],
+                    rhs=qc[b][:, cols].bitcast(FP8X4),
+                    rhs_scale=qs[b][:, cols],
+                    start=True,
+                    stop=True,
+                )
+
+        def gain(n, hh):
+            tt = work.tile([P, 4, P], F32, name="tg", bufs=3)
+            tg[n, hh] = tt
+            for tk in range(4):
+                j = hh * 4 + tk
+                nc.scalar.activation(out=tt[:, tk, :], in_=st[n, hh][:, tk, :], func=ACT.Copy, scale=gs[:, j : j + 1])
+
+        def weights(n, hh):
+            if hh == 0:
+                pt = work.tile([P, 2, 512], BF16, name="pb", bufs=3, align_bytes=64)
+                pb[n] = pt
+            nc.vector.scalar_tensor_tensor(
+                out=pb[n][:, hh, :].rearrange("p (i t) -> p i t", t=4),
+                in0=st[n, hh][:].rearrange("p t i -> p i t"),
+                scalar=0.0,
+                in1=tg[n, hh][:].rearrange("p t i -> p i t"),
+                op0=ALU.max,
+                op1=ALU.mult,
+            )
+
+        def quant_p(n):
+            ct = work.tile([P, 256], U32, name="pc", bufs=3, align_bytes=64)
+            pc[n] = ct
+            sct = work.tile([P, 256], U8, name="psc", bufs=3, align_bytes=64)
+            psc[n] = sct
+            nc.vector.quantize_mx(out=ct[:].bitcast(FP8X4), scales=sct[:], in_=pb[n][:].rearrange("p h x -> p (h x)"))
+
+        def st2(n, e):
+            b, h, t, cols = where(n)
+            bank = ps.tile([P, 512], F32, name="cb", bufs=2)
+            cb[n, e] = bank
+            for hh in range(2):
+                pcols = slice(hh * P, (hh + 1) * P)
+                ecols = slice(e * 512, (e + 1) * 512)
+                nc.tensor.matmul_mx(
+                    out=bank[:],
+                    lhsT=pc[n][:, pcols].bitcast(FP8X4),
+                    lhsT_scale=psc[n][:, pcols],
+                    rhs=vc[b, hh][:, ecols].bitcast(FP8X4),
+                    rhs_scale=vs[b, hh][:, ecols],
+                    start=(hh == 0),
+                    stop=(hh == 1),
+                )
+
+        def silu(n, e):
+            b, h, t, cols = where(n)
+            if e == 0:
+                gt = work.tile([P, E], F32, name="gate", bufs=3)
+                gate[n] = gt
+            nc.scalar.activation(out=gate[n][:, e * 512 : (e + 1) * 512], in_=u_sb[b, h][:, t, e * 512 : (e + 1) * 512], func=ACT.Silu)
+
+        def apply_gate(n, e):
+            if e == 0:
+                ot = work.tile([P, E], F32, name="o32", bufs=4)
+                o32[n] = ot
+            ecols = slice(e * 512, (e + 1) * 512)
+            nc.vector.tensor_tensor(out=o32[n][:, ecols], in0=cb[n, e][:], in1=gate[n][:, ecols], op=ALU.mult)
+
+        def store_out(n):
+            b, h, t, cols = where(n)
+            dst = out_0[b, h * 512 : (h + 1) * 512, :].rearrange("(m t) e -> m t e", t=4)[:, t, :]
+            nc.sync.dma_start(out=dst, in_=o32[n][:])
+
+        def round_out(n):
+            obt = work.tile([P, E], BF16, name="ob", bufs=4)
+            ob[n] = obt
+            nc.vector.tensor_copy(out=obt[:], in_=o32[n][:])
+
+        def turn(n, grp):
+            b, h, t, cols = where(n)
+            if t == 1 and grp == 0:
+                grt = work.tile([P, 2, 2048], BF16, name="gr", bufs=2, align_bytes=64)
+                gr[n // 4] = grt
+            bank = ps.tile([P, 2, 2, P], F32, name="tr", bufs=3)
+            for a in range(2):
+                words = ob[n - 1 + a][:].bitcast(F32)
+                for w in range(2):
+                    nc.tensor.transpose(bank[:, a, w, :], words[:, 256 * grp + w : 256 * (grp + 1) : 2], ident[:])
+            dst = gr[n // 4][:, grp, :].bitcast(F32).rearrange("p (m x) -> p m x", x=8)[:, :, 2 * (t - 1) : 2 * (t - 1) + 4]
+            nc.scalar.copy(out=dst, in_=bank[:].rearrange("p a w m -> p m (a w)"))
+
+        def quant_out(k, grp):
+            if grp == 0:
+                oct_ = work.tile([P, 2, 512], U32, name="oc", bufs=2, align_bytes=64)
+                oc[k] = oct_
+                ost = work.tile([P, 2, 512], U8, name="osc", bufs=2, align_bytes=64)
+                osc[k] = ost
+            nc.vector.quantize_mx(out=oc[k][:, grp, :].bitcast(FP8X4), scales=osc[k][:, grp, :], in_=gr[k][:, grp, :])
+
+        def store_planes(k):
+            tok = slice(k * 512, (k + 1) * 512)
+            for grp in range(2):
+                nc.sync.dma_start(
+                    out=out_1[grp, :, tok, :].rearrange("p m t -> p (m t)").bitcast(I32), in_=oc[k][:, grp, :].bitcast(I32)
+                )
+            for Q in range(4):
+                nc.sync.dma_start(
+                    out=out_2[:, 4 * Q : 4 * Q + 4, tok].rearrange("g q m -> q g m").bitcast(I32),
+                    in_=osc[k][32 * Q : 32 * Q + 4, :, :].bitcast(I32),
+                )
+
+        with tc.manual_schedule():
+            NT = 16
+            v_first = [(0, h, e4) for h in range(2) for e4 in range(4)]
+            v_second = [(1, h, e4) for h in range(2) for e4 in range(4)]
+
+            def do_v(item, engine="s"):
+                b, h, e4 = item
+                v_task(b, h, e4, engine)
+
+            for zb in range(4):
+                z_task(0, zb)
+                if zb > 0:
+                    quant_k(0, zb - 1)
+            do_v(v_first[0])
+            interleave_q(0, 0)
+            quant_k(0, 3)
+            interleave_q(0, 1)
+            quant_q(0, 0)
+            st1(0, 0)
+            gain(0, 0)
+            st1(0, 1)
+            gain(0, 1)
+            do_v(v_first[1])
+            interleave_q(0, 2)
+            quant_q(0, 1)
+            interleave_q(0, 3)
+            quant_q(0, 2)
+            weights(0, 0)
+            quant_q(0, 3)
+            weights(0, 1)
+            do_v(v_first[2])
+            do_v(v_first[3])
+            st1(1, 0)
+            gain(1, 0)
+            quant_v(0, 0, 0)
+            quant_p(0)
+            st1(1, 1)
+            gain(1, 1)
+            quant_v(0, 0, 1)
+            do_v(v_first[4])
+            do_v(v_first[5])
+            weights(1, 0)
+            do_v(v_first[6])
+            do_v(v_first[7])
+            weights(1, 1)
+            quant_v(0, 1, 0)
+            silu(0, 0)
+            silu(0, 1)
+            quant_v(0, 1, 1)
+            quant_p(1)
+
+            for s in range(NT + 2):
+                if s < NT:
+                    st2(s, 0)
+                    st2(s, 1)
+                if s + 2 < NT:
+                    st1(s + 2, 0)
+                    gain(s + 2, 0)
+                    st1(s + 2, 1)
+                    gain(s + 2, 1)
+                if s >= 2 and s % 2 == 0:
+                    turn(s - 1, 0)
+                    turn(s - 1, 1)
+                if s < NT:
+                    apply_gate(s, 0)
+                if s + 2 < NT:
+                    weights(s + 2, 0)
+                if s < NT:
+                    apply_gate(s, 1)
+                    store_out(s)
+                if s + 2 < NT:
+                    weights(s + 2, 1)
+                if s < NT:
+                    round_out(s)
+                if s + 1 < NT:
+                    silu(s + 1, 0)
+                    silu(s + 1, 1)
+                if s + 2 < NT:
+                    quant_p(s + 2)
+                if s >= 4 and s % 4 == 0:
+                    quant_out(s // 4 - 1, 0)
+                    quant_out(s // 4 - 1, 1)
+                    store_planes(s // 4 - 1)
+                if s < 6:
+                    if s < 4:
+                        z_task(1, s)
+                    if 1 <= s < 5:
+                        quant_k(1, s - 1)
+                        interleave_q(1, s - 1)
+                    if 2 <= s < 6:
+                        quant_q(1, s - 2)
+                if s < 8:
+                    do_v(v_second[s])
+                    if s % 2 == 1:
+                        quant_v(1, s // 4, (s // 2) % 2)

@@ -43,7 +43,7 @@ def tile_gatedattentionunitsquaredrelu_x1_kernel(tc, z, gq, cq, gk, g, v, u, out
                 nc.sync.dma_start(out=z_sb[b, h][:, i * w : (i + 1) * w, :], in_=src[:, i * w : (i + 1) * w, :])
 
         def load_rows(store, src, name, b, h):
-            store[b, h] = const.tile([P, 4, E], BF16, name="%s%d%d" % (name, b, h))
+            store[b, h] = const.tile([P, 4, E], BF16, name=name, bufs=3)
             nc.sync.dma_start(out=store[b, h][:], in_=src[b, h * 512 : (h + 1) * 512, :].rearrange("(m t) e -> m t e", t=4))
 
         load_z(0, 0, 2)
@@ -55,9 +55,6 @@ def tile_gatedattentionunitsquaredrelu_x1_kernel(tc, z, gq, cq, gk, g, v, u, out
         load_z(1, 1, 1)
         load_rows(u_sb, u, "u", 0, 1)
         load_rows(v_sb, v, "v", 1, 0)
-        load_rows(v_sb, v, "v", 1, 1)
-        load_rows(u_sb, u, "u", 1, 0)
-        load_rows(u_sb, u, "u", 1, 1)
 
         warm = const.tile([P, 1], F32, name="warm")
         nc.vector.memset(warm[:], 0.0)
@@ -65,14 +62,29 @@ def tile_gatedattentionunitsquaredrelu_x1_kernel(tc, z, gq, cq, gk, g, v, u, out
         nc.scalar.activation(out=warm2[:], in_=warm[:], func=ACT.Silu)
         ident = const.tile([P, P], F32, name="ident")
         make_identity(nc, ident[:])
-        identb = const.tile([P, P], BF16, name="identb")
-        make_identity(nc, identb[:])
         gq32 = const.tile([P, 4], F32, name="gq32")
         cq32 = const.tile([P, 4], F32, name="cq32")
-        gs = const.tile([P, 8], F32, name="gs")
+        gf = g_raw[:].rearrange("p h t -> p (h t)")
+        neg = const.tile([P, 8], F32, name="neg")
+        mag = const.tile([P, 8], F32, name="mag")
+        half = const.tile([P, 8], F32, name="half")
+        root = const.tile([P, 8], F32, name="root")
+        rs = const.tile([P, 8], F32, name="rs")
+        step = const.tile([P, 8], F32, name="step")
+        sgn = const.tile([P, 8], F32, name="sgn")
+        nc.gpsimd.memset(half[:], 0.5)
         nc.vector.tensor_copy(out=gq32[:], in_=gq_raw[:])
         nc.vector.tensor_copy(out=cq32[:], in_=cq_raw[:])
-        nc.vector.tensor_scalar(out=gs[:], in0=g_raw[:].rearrange("p h t -> p (h t)"), scalar1=1.0 / 4096.0, scalar2=None, op0=ALU.mult)
+        nc.vector.tensor_scalar(out=neg[:], in0=gf, scalar1=-1.0, scalar2=None, op0=ALU.mult)
+        nc.vector.tensor_scalar(out=step[:], in0=gf, scalar1=0.0, scalar2=2.0, op0=ALU.is_ge, op1=ALU.mult)
+        nc.vector.tensor_tensor(out=mag[:], in0=neg[:], in1=gf, op=ALU.max)
+        nc.vector.tensor_scalar(out=sgn[:], in0=step[:], scalar1=-1.0, scalar2=None, op0=ALU.add)
+        nc.gpsimd.tensor_tensor(out=root[:], in0=mag[:], in1=half[:], op=ALU.pow)
+        nc.gpsimd.tensor_scalar(out=rs[:], in0=root[:], scalar1=1.0 / 64.0, scalar2=0.0, op0=ALU.mult, op1=ALU.add)
+        sgnb = const.tile([P, 4 * 2], BF16, name="sgnb")
+        nc.vector.tensor_copy(out=sgnb[:], in_=sgn[:])
+        identb = const.tile([P, P], BF16, name="identb")
+        nc.vector.tensor_copy(out=identb[:], in_=ident[:])
 
         kc, ks, qc, qs, vc, vs = {}, {}, {}, {}, {}, {}
         for b in range(B):
@@ -86,114 +98,141 @@ def tile_gatedattentionunitsquaredrelu_x1_kernel(tc, z, gq, cq, gk, g, v, u, out
 
         kb, qp, qb = {}, {}, {}
 
-        def z_task(b, zb):
+        zt = {}
+
+        def z_turn(b, zb):
             h, tp = divmod(zb, 2)
-            bank = ps.tile([P, 2, 2, P], F32, name="tr", bufs=3)
+            bank = ps.tile([P, 2, 2, P], F32, name="st", bufs=4)
             words = z_sb[b, h][:].rearrange("p t c -> p (t c)").bitcast(F32)
             for a in range(2):
                 t = 2 * tp + a
                 for w in range(2):
                     nc.tensor.transpose(bank[:, w, a, :], words[:, 256 * t + w : 256 * (t + 1) : 2], ident[:])
-            zv = bank[:].rearrange("p w a m -> p (w a m)").bitcast(BF16).rearrange("p (w i e) -> p w i e", w=2, e=2)
-            kt = work.tile([P, 1024], BF16, name="kb", bufs=3, align_bytes=64)
-            kb[b, zb] = kt
+            zt[b, zb] = bank[:].rearrange("p w a m -> p (w a m)").bitcast(BF16).rearrange("p (w i e) -> p w i e", w=2, e=2)
+
+        def k_make(b, zb):
+            h, tp = divmod(zb, 2)
+            if tp == 0:
+                kt = work.tile([P, 2, 1024], BF16, name="kb", bufs=2, align_bytes=64)
+                kb[b, h] = kt
             nc.vector.tensor_tensor(
-                out=kt[:].rearrange("p (i w e) -> p i w e", w=2, e=2),
-                in0=zv.rearrange("p w i e -> p i w e"),
+                out=kb[b, h][:, tp, :].rearrange("p (i w e) -> p i w e", w=2, e=2),
+                in0=zt[b, zb].rearrange("p w i e -> p i w e"),
                 in1=gk_raw[:].rearrange("p (w e) -> p w e", e=2).unsqueeze(1).to_broadcast([P, 256, 2, 2]),
                 op=ALU.mult,
             )
-            qt = work.tile([P, 32, 4, 8], BF16, name="qp", bufs=2)
-            qp[b, zb] = qt
+
+        def q_make(b, zb):
+            h, tp = divmod(zb, 2)
+            if tp == 0:
+                qt = work.tile([P, 2, 32, 4, 8], BF16, name="qp", bufs=2)
+                qp[b, h] = qt
             for t in range(4):
                 w, e = divmod(t, 2)
                 nc.scalar.activation(
-                    out=qt[:, :, t, :],
-                    in_=zv[:, w, :, e].rearrange("p (c i) -> p c i", i=8),
+                    out=qp[b, h][:, tp, :, t, :],
+                    in_=zt[b, zb][:, w, :, e].rearrange("p (c i) -> p c i", i=8),
                     func=ACT.Identity,
                     scale=gq32[:, t : t + 1],
                     bias=cq32[:, t : t + 1],
                 )
 
-        def quant_k(b, zb):
-            cols = slice(zb * 256, (zb + 1) * 256)
-            nc.vector.quantize_mx(out=kc[b][:, cols].bitcast(FP8X4), scales=ks[b][:, cols], in_=kb[b, zb][:])
-
-        def interleave_q(b, zb):
-            qt = work.tile([P, 1024], BF16, name="qb", bufs=3, align_bytes=64)
-            qb[b, zb] = qt
-            nc.vector.tensor_copy(
-                out=qt[:].rearrange("p (c i t) -> p c i t", i=8, t=4), in_=qp[b, zb][:].rearrange("p c t i -> p c i t")
+        def quant_k(b, h):
+            cols = slice(h * 512, (h + 1) * 512)
+            nc.vector.quantize_mx(
+                out=kc[b][:, cols].bitcast(FP8X4), scales=ks[b][:, cols], in_=kb[b, h][:].rearrange("p a x -> p (a x)")
             )
 
-        def quant_q(b, zb):
-            cols = slice(zb * 256, (zb + 1) * 256)
-            nc.vector.quantize_mx(out=qc[b][:, cols].bitcast(FP8X4), scales=qs[b][:, cols], in_=qb[b, zb][:])
+        def interleave_q(b, h):
+            qt = work.tile([P, 2048], BF16, name="qb", bufs=2, align_bytes=64)
+            qb[b, h] = qt
+            nc.vector.tensor_copy(
+                out=qt[:].rearrange("p (c i t) -> p c i t", i=8, t=4),
+                in_=qp[b, h][:].rearrange("p a c t i -> p (a c) i t"),
+            )
+
+        def quant_q(b, h):
+            cols = slice(h * 512, (h + 1) * 512)
+            nc.vector.quantize_mx(out=qc[b][:, cols].bitcast(FP8X4), scales=qs[b][:, cols], in_=qb[b, h][:])
 
         vb = {}
 
-        def v_task(b, h, e4, engine):
-            bank = ps.tile([P, 4, 256], BF16, name="tr", bufs=3)
-            for t in range(4):
-                nc.tensor.matmul(bank[:, t, :], lhsT=identb[:], rhs=v_sb[b, h][:, t, e4 * 256 : (e4 + 1) * 256], start=True, stop=True)
+        vt_bank = {}
+
+        def v_turn(b, h, e4):
+            bank = ps.tile([P, 256, 4], BF16, name="tr", bufs=2)
+            vt_bank[b, h, e4] = bank
+            for i in range(2):
+                e0 = e4 * 256 + i * 128
+                nc.tensor.matmul(
+                    bank[:, i * 128 : (i + 1) * 128, :],
+                    lhsT=identb[:],
+                    rhs=v_sb[b, h][:, :, e0 : e0 + 128].rearrange("p t e -> p e t"),
+                    start=True,
+                    stop=True,
+                )
+
+        def v_copy(b, h, e4):
             if e4 % 2 == 0:
                 vt = work.tile([P, 2, 1024], BF16, name="vb", bufs=2, align_bytes=64)
                 vb[b, h, e4 // 2] = vt
-            dst = vb[b, h, e4 // 2][:, e4 % 2, :].rearrange("p (i t) -> p i t", t=4)
-            src = bank[:].rearrange("p t i -> p i t")
-            if engine == "s":
-                nc.scalar.copy(out=dst, in_=src)
-            else:
-                nc.vector.tensor_copy(out=dst, in_=src)
+            nc.vector.tensor_tensor(
+                out=vb[b, h, e4 // 2][:, e4 % 2, :].rearrange("p (e t) -> p e t", t=4),
+                in0=vt_bank[b, h, e4][:],
+                in1=sgnb[:, h * 4 : (h + 1) * 4].unsqueeze(1).to_broadcast([P, 256, 4]),
+                op=ALU.mult,
+            )
 
         def quant_v(b, h, e2):
             cols = slice(e2 * 512, (e2 + 1) * 512)
-            nc.vector.quantize_mx(
-                out=vc[b, h][:, cols].bitcast(FP8X4), scales=vs[b, h][:, cols], in_=vb[b, h, e2][:].rearrange("p a x -> p (a x)")
-            )
+            nc.vector.quantize_mx(out=vc[b, h][:, cols].bitcast(FP8X4), scales=vs[b, h][:, cols], in_=vb[b, h, e2][:].rearrange("p a x -> p (a x)"))
 
         def where(n):
             b, r = divmod(n, 8)
             h, t = divmod(r, 4)
             return b, h, t, slice(r * P, (r + 1) * P)
 
-        st, tg, pb, pc, psc, cb, gate, o32, ob, gr, oc, osc = {}, {}, {}, {}, {}, {}, {}, {}, {}, {}, {}, {}
+        turned, sc = {}, {}
+        xr, pb, pc, psc, cb, gate, o32, ob, gr, oc, osc = {}, {}, {}, {}, {}, {}, {}, {}, {}, {}, {}
 
-        def st1(n, hh):
-            b, h, t, cols = where(n)
-            bank = ps.tile([P, 4, P], F32, name="st", bufs=3)
-            st[n, hh] = bank
-            for tk in range(4):
-                kcols = slice(hh * 512 + tk * P, hh * 512 + (tk + 1) * P)
-                nc.tensor.matmul_mx(
-                    out=bank[:, tk, :],
-                    lhsT=kc[b][:, kcols].bitcast(FP8X4),
-                    lhsT_scale=ks[b][:, kcols],
-                    rhs=qc[b][:, cols].bitcast(FP8X4),
-                    rhs_scale=qs[b][:, cols],
-                    start=True,
-                    stop=True,
-                )
-
-        def gain(n, hh):
-            tt = work.tile([P, 4, P], F32, name="tg", bufs=3)
-            tg[n, hh] = tt
-            for tk in range(4):
-                j = hh * 4 + tk
-                nc.scalar.activation(out=tt[:, tk, :], in_=st[n, hh][:, tk, :], func=ACT.Copy, scale=gs[:, j : j + 1])
-
-        def weights(n, hh):
-            if hh == 0:
-                pt = work.tile([P, 2, 512], BF16, name="pb", bufs=3, align_bytes=64)
-                pb[n] = pt
-            nc.vector.scalar_tensor_tensor(
-                out=pb[n][:, hh, :].rearrange("p (i t) -> p i t", t=4),
-                in0=st[n, hh][:].rearrange("p t i -> p i t"),
-                scalar=0.0,
-                in1=tg[n, hh][:].rearrange("p t i -> p i t"),
-                op0=ALU.max,
-                op1=ALU.mult,
+        def scores(k, hh, tk):
+            b, h = divmod(k, 2)
+            bank = ps.tile([P, 512], F32, name="st", bufs=4)
+            sc[k, hh, tk] = bank
+            kcols = slice(hh * 512 + tk * P, hh * 512 + (tk + 1) * P)
+            qcols = slice(h * 512, (h + 1) * 512)
+            nc.tensor.matmul_mx(
+                out=bank[:],
+                lhsT=kc[b][:, kcols].bitcast(FP8X4),
+                lhsT_scale=ks[b][:, kcols],
+                rhs=qc[b][:, qcols].bitcast(FP8X4),
+                rhs_scale=qs[b][:, qcols],
+                start=True,
+                stop=True,
             )
+
+        def relu_root(k, hh, tk, engine):
+            if (hh, tk) == (0, 0):
+                xt = work.tile([P, 4, 2, 32, 4, 4], F32, name="xt", bufs=2)
+                xr[k] = xt
+            j = hh * 4 + tk
+            dst = xr[k][:, :, hh, :, tk, :]
+            src = sc[k, hh, tk][:].rearrange("p (a c i) -> p a c i", a=4, i=4)
+            if engine == "s":
+                nc.scalar.activation(out=dst, in_=src, func=ACT.Relu, scale=rs[:, j : j + 1])
+            else:
+                nc.vector.tensor_scalar(out=dst, in0=src, scalar1=rs[:, j : j + 1], scalar2=0.0, op0=ALU.mult, op1=ALU.max)
+
+        def square(n, engine):
+            k, a = divmod(n, 4)
+            pt = work.tile([P, 2, 512], BF16, name="pb", bufs=3, align_bytes=64)
+            pb[n] = pt
+            dst = pt[:].rearrange("p h (c i t) -> p (h c) t i", i=4, t=4)
+            src = xr[k][:, a].rearrange("p h c t i -> p (h c) t i")
+            if engine == "s":
+                nc.scalar.activation(out=dst, in_=src, func=ACT.Square)
+            else:
+                nc.vector.tensor_tensor(out=dst, in0=src, in1=src, op=ALU.mult)
 
         def quant_p(n):
             ct = work.tile([P, 256], U32, name="pc", bufs=3, align_bytes=64)
@@ -219,12 +258,11 @@ def tile_gatedattentionunitsquaredrelu_x1_kernel(tc, z, gq, cq, gk, g, v, u, out
                     stop=(hh == 1),
                 )
 
-        def silu(n, e):
+        def silu(n):
             b, h, t, cols = where(n)
-            if e == 0:
-                gt = work.tile([P, E], F32, name="gate", bufs=3)
-                gate[n] = gt
-            nc.scalar.activation(out=gate[n][:, e * 512 : (e + 1) * 512], in_=u_sb[b, h][:, t, e * 512 : (e + 1) * 512], func=ACT.Silu)
+            gt = work.tile([P, E], F32, name="gate", bufs=3)
+            gate[n] = gt
+            nc.scalar.activation(out=gt[:], in_=u_sb[b, h][:, t, :], func=ACT.Silu)
 
         def apply_gate(n, e):
             if e == 0:
@@ -239,22 +277,26 @@ def tile_gatedattentionunitsquaredrelu_x1_kernel(tc, z, gq, cq, gk, g, v, u, out
             nc.sync.dma_start(out=dst, in_=o32[n][:])
 
         def round_out(n):
-            obt = work.tile([P, E], BF16, name="ob", bufs=4)
+            obt = work.tile([P, E], BF16, name="ob", bufs=3)
             ob[n] = obt
             nc.vector.tensor_copy(out=obt[:], in_=o32[n][:])
 
         def turn(n, grp):
             b, h, t, cols = where(n)
-            if t == 1 and grp == 0:
-                grt = work.tile([P, 2, 2048], BF16, name="gr", bufs=2, align_bytes=64)
-                gr[n // 4] = grt
-            bank = ps.tile([P, 2, 2, P], F32, name="tr", bufs=3)
+            if t == 1:
+                grt = work.tile([P, 2048], BF16, name="gr", bufs=3, align_bytes=64)
+                gr[n // 4, grp] = grt
+            bank = ps.tile([P, 2, 2, P], F32, name="tr", bufs=2)
             for a in range(2):
                 words = ob[n - 1 + a][:].bitcast(F32)
                 for w in range(2):
                     nc.tensor.transpose(bank[:, a, w, :], words[:, 256 * grp + w : 256 * (grp + 1) : 2], ident[:])
-            dst = gr[n // 4][:, grp, :].bitcast(F32).rearrange("p (m x) -> p m x", x=8)[:, :, 2 * (t - 1) : 2 * (t - 1) + 4]
-            nc.scalar.copy(out=dst, in_=bank[:].rearrange("p a w m -> p m (a w)"))
+            turned[n, grp] = bank
+
+        def turn_copy(n, grp):
+            b, h, t, cols = where(n)
+            dst = gr[n // 4, grp][:].bitcast(F32).rearrange("p (m x) -> p m x", x=8)[:, :, 2 * (t - 1) : 2 * (t - 1) + 4]
+            nc.scalar.copy(out=dst, in_=turned[n, grp][:].rearrange("p a w m -> p m (a w)"))
 
         def quant_out(k, grp):
             if grp == 0:
@@ -262,7 +304,7 @@ def tile_gatedattentionunitsquaredrelu_x1_kernel(tc, z, gq, cq, gk, g, v, u, out
                 oc[k] = oct_
                 ost = work.tile([P, 2, 512], U8, name="osc", bufs=2, align_bytes=64)
                 osc[k] = ost
-            nc.vector.quantize_mx(out=oc[k][:, grp, :].bitcast(FP8X4), scales=osc[k][:, grp, :], in_=gr[k][:, grp, :])
+            nc.vector.quantize_mx(out=oc[k][:, grp, :].bitcast(FP8X4), scales=osc[k][:, grp, :], in_=gr[k, grp][:])
 
         def store_planes(k):
             tok = slice(k * 512, (k + 1) * 512)
@@ -277,97 +319,334 @@ def tile_gatedattentionunitsquaredrelu_x1_kernel(tc, z, gq, cq, gk, g, v, u, out
                 )
 
         with tc.manual_schedule():
-            NT = 16
-            v_first = [(0, h, e4) for h in range(2) for e4 in range(4)]
-            v_second = [(1, h, e4) for h in range(2) for e4 in range(4)]
-
-            def do_v(item, engine="s"):
-                b, h, e4 = item
-                v_task(b, h, e4, engine)
-
-            for zb in range(4):
-                z_task(0, zb)
-                if zb > 0:
-                    quant_k(0, zb - 1)
-            do_v(v_first[0])
+            load_rows(u_sb, u, "u", 1, 0)
+            z_turn(0, 0)
+            z_turn(0, 1)
+            q_make(0, 0)
+            k_make(0, 0)
+            z_turn(0, 2)
+            k_make(0, 1)
+            z_turn(0, 3)
+            k_make(0, 2)
+            q_make(0, 1)
+            k_make(0, 3)
+            quant_k(0, 0)
+            v_turn(0, 0, 0)
+            q_make(0, 2)
             interleave_q(0, 0)
-            quant_k(0, 3)
-            interleave_q(0, 1)
+            v_turn(0, 0, 1)
+            q_make(0, 3)
+            quant_k(0, 1)
             quant_q(0, 0)
-            st1(0, 0)
-            gain(0, 0)
-            st1(0, 1)
-            gain(0, 1)
-            do_v(v_first[1])
-            interleave_q(0, 2)
+            interleave_q(0, 1)
+            scores(0, 0, 0)
+            scores(0, 0, 1)
+            relu_root(0, 0, 0, "s")
+            scores(0, 0, 2)
+            scores(0, 0, 3)
+            v_copy(0, 0, 0)
+            relu_root(0, 0, 1, "s")
+            scores(0, 1, 0)
             quant_q(0, 1)
-            interleave_q(0, 3)
-            quant_q(0, 2)
-            weights(0, 0)
-            quant_q(0, 3)
-            weights(0, 1)
-            do_v(v_first[2])
-            do_v(v_first[3])
-            st1(1, 0)
-            gain(1, 0)
+            relu_root(0, 0, 2, "s")
+            v_turn(0, 1, 0)
+            v_copy(0, 0, 1)
+            relu_root(0, 0, 3, "s")
+            relu_root(0, 1, 0, "s")
+            scores(0, 1, 1)
             quant_v(0, 0, 0)
-            quant_p(0)
-            st1(1, 1)
-            gain(1, 1)
-            quant_v(0, 0, 1)
-            do_v(v_first[4])
-            do_v(v_first[5])
-            weights(1, 0)
-            do_v(v_first[6])
-            do_v(v_first[7])
-            weights(1, 1)
+            scores(0, 1, 2)
+            silu(0)
+            v_copy(0, 1, 0)
+            scores(0, 1, 3)
+            scores(1, 0, 0)
+            v_turn(0, 1, 1)
+            relu_root(0, 1, 1, "s")
+            relu_root(0, 1, 2, "s")
+            v_turn(0, 0, 2)
+            v_copy(0, 1, 1)
+            relu_root(0, 1, 3, "s")
+            relu_root(1, 0, 0, "s")
             quant_v(0, 1, 0)
-            silu(0, 0)
-            silu(0, 1)
-            quant_v(0, 1, 1)
+            v_turn(0, 0, 3)
+            square(0, "s")
+            v_copy(0, 0, 2)
+            z_turn(1, 0)
+            v_copy(0, 0, 3)
+            load_rows(v_sb, v, "v", 1, 1)
+            square(1, "s")
+            v_turn(0, 1, 2)
+            quant_p(0)
+            quant_v(0, 0, 1)
+            q_make(1, 0)
+            k_make(1, 0)
+            v_turn(0, 1, 3)
+            v_copy(0, 1, 2)
+            scores(1, 0, 1)
             quant_p(1)
-
-            for s in range(NT + 2):
-                if s < NT:
-                    st2(s, 0)
-                    st2(s, 1)
-                if s + 2 < NT:
-                    st1(s + 2, 0)
-                    gain(s + 2, 0)
-                    st1(s + 2, 1)
-                    gain(s + 2, 1)
-                if s >= 2 and s % 2 == 0:
-                    turn(s - 1, 0)
-                    turn(s - 1, 1)
-                if s < NT:
-                    apply_gate(s, 0)
-                if s + 2 < NT:
-                    weights(s + 2, 0)
-                if s < NT:
-                    apply_gate(s, 1)
-                    store_out(s)
-                if s + 2 < NT:
-                    weights(s + 2, 1)
-                if s < NT:
-                    round_out(s)
-                if s + 1 < NT:
-                    silu(s + 1, 0)
-                    silu(s + 1, 1)
-                if s + 2 < NT:
-                    quant_p(s + 2)
-                if s >= 4 and s % 4 == 0:
-                    quant_out(s // 4 - 1, 0)
-                    quant_out(s // 4 - 1, 1)
-                    store_planes(s // 4 - 1)
-                if s < 6:
-                    if s < 4:
-                        z_task(1, s)
-                    if 1 <= s < 5:
-                        quant_k(1, s - 1)
-                        interleave_q(1, s - 1)
-                    if 2 <= s < 6:
-                        quant_q(1, s - 2)
-                if s < 8:
-                    do_v(v_second[s])
-                    if s % 2 == 1:
-                        quant_v(1, s // 4, (s // 2) % 2)
+            silu(1)
+            v_copy(0, 1, 3)
+            z_turn(1, 1)
+            scores(1, 0, 2)
+            quant_v(0, 1, 1)
+            relu_root(1, 0, 1, "s")
+            z_turn(1, 2)
+            q_make(1, 1)
+            k_make(1, 1)
+            scores(1, 0, 3)
+            k_make(1, 2)
+            st2(0, 0)
+            st2(0, 1)
+            quant_k(1, 0)
+            q_make(1, 2)
+            scores(1, 1, 0)
+            interleave_q(1, 0)
+            v_turn(1, 0, 0)
+            relu_root(1, 0, 2, "s")
+            apply_gate(0, 0)
+            scores(1, 1, 1)
+            relu_root(1, 0, 3, "s")
+            z_turn(1, 3)
+            apply_gate(0, 1)
+            square(2, "s")
+            st2(1, 0)
+            v_copy(1, 0, 0)
+            store_out(0)
+            st2(1, 1)
+            round_out(0)
+            q_make(1, 3)
+            scores(1, 1, 2)
+            k_make(1, 3)
+            v_turn(1, 0, 1)
+            quant_p(2)
+            relu_root(1, 1, 0, "s")
+            apply_gate(1, 0)
+            relu_root(1, 1, 1, "s")
+            interleave_q(1, 1)
+            scores(1, 1, 3)
+            st2(2, 0)
+            silu(2)
+            apply_gate(1, 1)
+            square(3, "s")
+            quant_q(1, 0)
+            store_out(1)
+            st2(2, 1)
+            round_out(1)
+            relu_root(1, 1, 2, "s")
+            scores(2, 0, 0)
+            scores(2, 0, 1)
+            v_copy(1, 0, 1)
+            relu_root(1, 1, 3, "s")
+            turn(1, 0)
+            quant_q(1, 1)
+            silu(3)
+            v_turn(1, 1, 0)
+            quant_v(1, 0, 0)
+            quant_p(3)
+            square(4, "s")
+            load_rows(u_sb, u, "u", 1, 1)
+            scores(2, 0, 2)
+            apply_gate(2, 0)
+            scores(2, 0, 3)
+            apply_gate(2, 1)
+            st2(3, 0)
+            turn_copy(1, 0)
+            v_copy(1, 1, 0)
+            store_out(2)
+            st2(3, 1)
+            relu_root(2, 0, 0, "s")
+            round_out(2)
+            turn(1, 1)
+            silu(4)
+            quant_p(4)
+            v_turn(1, 1, 1)
+            apply_gate(3, 0)
+            relu_root(2, 0, 1, "s")
+            apply_gate(3, 1)
+            relu_root(2, 0, 2, "s")
+            st2(4, 0)
+            square(5, "v")
+            store_out(3)
+            turn_copy(1, 1)
+            st2(4, 1)
+            silu(5)
+            round_out(3)
+            v_turn(1, 0, 2)
+            v_copy(1, 1, 1)
+            relu_root(2, 0, 3, "s")
+            quant_k(1, 1)
+            v_turn(1, 0, 3)
+            square(6, "s")
+            quant_v(1, 1, 0)
+            quant_p(5)
+            scores(2, 1, 0)
+            v_copy(1, 0, 2)
+            silu(6)
+            scores(2, 1, 1)
+            scores(2, 1, 2)
+            apply_gate(4, 0)
+            scores(2, 1, 3)
+            turn(3, 0)
+            relu_root(2, 1, 0, "s")
+            apply_gate(4, 1)
+            st2(5, 0)
+            relu_root(2, 1, 1, "s")
+            quant_p(6)
+            store_out(4)
+            round_out(4)
+            st2(5, 1)
+            turn_copy(3, 0)
+            v_copy(1, 0, 3)
+            scores(3, 0, 0)
+            square(7, "s")
+            scores(3, 0, 1)
+            apply_gate(5, 0)
+            turn(3, 1)
+            quant_v(1, 0, 1)
+            v_turn(1, 1, 2)
+            relu_root(2, 1, 2, "s")
+            apply_gate(5, 1)
+            relu_root(2, 1, 3, "s")
+            quant_p(7)
+            st2(6, 0)
+            turn_copy(3, 1)
+            store_out(5)
+            round_out(5)
+            st2(6, 1)
+            silu(7)
+            v_copy(1, 1, 2)
+            turn(5, 0)
+            apply_gate(6, 0)
+            square(8, "s")
+            v_turn(1, 1, 3)
+            apply_gate(6, 1)
+            square(9, "v")
+            store_out(6)
+            turn_copy(5, 0)
+            st2(7, 0)
+            relu_root(3, 0, 0, "s")
+            st2(7, 1)
+            round_out(6)
+            silu(8)
+            scores(3, 0, 2)
+            quant_p(8)
+            scores(3, 0, 3)
+            v_copy(1, 1, 3)
+            scores(3, 1, 0)
+            relu_root(3, 0, 1, "s")
+            apply_gate(7, 0)
+            turn(5, 1)
+            relu_root(3, 0, 2, "s")
+            quant_v(1, 1, 1)
+            st2(8, 0)
+            silu(9)
+            apply_gate(7, 1)
+            scores(3, 1, 1)
+            quant_p(9)
+            scores(3, 1, 2)
+            store_out(7)
+            st2(8, 1)
+            round_out(7)
+            relu_root(3, 0, 3, "s")
+            apply_gate(8, 0)
+            square(10, "s")
+            turn(7, 0)
+            apply_gate(8, 1)
+            st2(9, 0)
+            quant_out(0, 0)
+            relu_root(3, 1, 0, "s")
+            store_out(8)
+            st2(9, 1)
+            round_out(8)
+            turn_copy(7, 0)
+            scores(3, 1, 3)
+            quant_p(10)
+            turn_copy(5, 1)
+            apply_gate(9, 0)
+            relu_root(3, 1, 1, "s")
+            turn(7, 1)
+            apply_gate(9, 1)
+            silu(10)
+            st2(10, 0)
+            quant_out(0, 1)
+            store_out(9)
+            st2(10, 1)
+            round_out(9)
+            square(11, "s")
+            store_planes(0)
+            apply_gate(10, 0)
+            turn(9, 0)
+            apply_gate(10, 1)
+            relu_root(3, 1, 2, "s")
+            quant_p(11)
+            relu_root(3, 1, 3, "s")
+            store_out(10)
+            round_out(10)
+            st2(11, 0)
+            turn_copy(7, 1)
+            square(13, "v")
+            st2(11, 1)
+            silu(11)
+            turn(9, 1)
+            quant_out(1, 0)
+            square(12, "s")
+            apply_gate(11, 0)
+            apply_gate(11, 1)
+            turn_copy(9, 0)
+            quant_p(12)
+            store_out(11)
+            round_out(11)
+            silu(12)
+            st2(12, 0)
+            quant_p(13)
+            st2(12, 1)
+            quant_out(1, 1)
+            turn_copy(9, 1)
+            turn(11, 0)
+            apply_gate(12, 0)
+            silu(13)
+            store_planes(1)
+            turn(11, 1)
+            apply_gate(12, 1)
+            st2(13, 0)
+            square(14, "s")
+            round_out(12)
+            store_out(12)
+            st2(13, 1)
+            apply_gate(13, 0)
+            turn_copy(11, 0)
+            quant_p(14)
+            apply_gate(13, 1)
+            silu(14)
+            st2(14, 0)
+            quant_out(2, 0)
+            store_out(13)
+            st2(14, 1)
+            square(15, "s")
+            round_out(13)
+            apply_gate(14, 0)
+            turn(13, 0)
+            turn_copy(11, 1)
+            apply_gate(14, 1)
+            silu(15)
+            quant_p(15)
+            turn(13, 1)
+            store_out(14)
+            round_out(14)
+            st2(15, 0)
+            quant_out(2, 1)
+            turn_copy(13, 0)
+            st2(15, 1)
+            apply_gate(15, 0)
+            turn_copy(13, 1)
+            store_planes(2)
+            apply_gate(15, 1)
+            round_out(15)
+            store_out(15)
+            turn(15, 0)
+            turn(15, 1)
+            turn_copy(15, 0)
+            turn_copy(15, 1)
+            quant_out(3, 0)
+            quant_out(3, 1)
+            store_planes(3)

@@ -36,7 +36,7 @@ def tile_gatedattentionunitsquaredrelu_x1_kernel(tc, z, gq, cq, gk, g, v, u, out
         z_sb, v_sb, u_sb = {}, {}, {}
 
         def load_z(b, h, parts):
-            z_sb[b, h] = const.tile([P, 4, Z], BF16, name="z%d%d" % (b, h))
+            z_sb[b, h] = const.tile([P, 4, Z], BF16, name="z", bufs=3)
             src = z[b, h * 512 : (h + 1) * 512, :].rearrange("(m t) c -> m t c", t=4)
             w = 4 // parts
             for i in range(parts):
@@ -52,9 +52,6 @@ def tile_gatedattentionunitsquaredrelu_x1_kernel(tc, z, gq, cq, gk, g, v, u, out
         load_rows(v_sb, v, "v", 0, 1)
         load_rows(u_sb, u, "u", 0, 0)
         load_z(1, 0, 1)
-        load_z(1, 1, 1)
-        load_rows(u_sb, u, "u", 0, 1)
-        load_rows(v_sb, v, "v", 1, 0)
 
         warm = const.tile([P, 1], F32, name="warm")
         nc.vector.memset(warm[:], 0.0)
@@ -102,7 +99,7 @@ def tile_gatedattentionunitsquaredrelu_x1_kernel(tc, z, gq, cq, gk, g, v, u, out
 
         def z_turn(b, zb):
             h, tp = divmod(zb, 2)
-            bank = ps.tile([P, 2, 2, P], F32, name="st", bufs=4)
+            bank = ps.tile([P, 2, 2, P], F32, name="st", bufs=3)
             words = z_sb[b, h][:].rearrange("p t c -> p (t c)").bitcast(F32)
             for a in range(2):
                 t = 2 * tp + a
@@ -112,7 +109,7 @@ def tile_gatedattentionunitsquaredrelu_x1_kernel(tc, z, gq, cq, gk, g, v, u, out
 
         def k_make(b, zb):
             h, tp = divmod(zb, 2)
-            if tp == 0:
+            if (b, h) not in kb:
                 kt = work.tile([P, 2, 1024], BF16, name="kb", bufs=2, align_bytes=64)
                 kb[b, h] = kt
             nc.vector.tensor_tensor(
@@ -124,7 +121,7 @@ def tile_gatedattentionunitsquaredrelu_x1_kernel(tc, z, gq, cq, gk, g, v, u, out
 
         def q_make(b, zb):
             h, tp = divmod(zb, 2)
-            if tp == 0:
+            if (b, h) not in qp:
                 qt = work.tile([P, 2, 32, 4, 8], BF16, name="qp", bufs=2)
                 qp[b, h] = qt
             for t in range(4):
@@ -137,43 +134,77 @@ def tile_gatedattentionunitsquaredrelu_x1_kernel(tc, z, gq, cq, gk, g, v, u, out
                     bias=cq32[:, t : t + 1],
                 )
 
+        zp = {}
+
+        def zq_turn(b, h, tp):
+            bank = ps.tile([P, 2, 4, P], BF16, name="tr", bufs=3)
+            zp[b, h, tp] = bank
+            for i in range(2):
+                for a in range(4):
+                    nc.tensor.transpose(bank[:, i, a, :], z_sb[b, h][:, a, 2 * tp + i : Z : 4], identb[:])
+
+        def q_plane(b, h, t):
+            if (b, h) not in qp:
+                qt = work.tile([P, 2, 32, 4, 8], BF16, name="qp", bufs=2)
+                qp[b, h] = qt
+            nc.vector.tensor_scalar(
+                out=qp[b, h][:, :, :, t, :].rearrange("p a c i -> p (a c) i"),
+                in0=zp[b, h, t // 2][:, t % 2].rearrange("p a m -> p (a m)").rearrange("p (c i) -> p c i", i=8),
+                scalar1=gq32[:, t : t + 1],
+                scalar2=cq32[:, t : t + 1],
+                op0=ALU.mult,
+                op1=ALU.add,
+            )
+
         def quant_k(b, h):
             cols = slice(h * 512, (h + 1) * 512)
             nc.vector.quantize_mx(
                 out=kc[b][:, cols].bitcast(FP8X4), scales=ks[b][:, cols], in_=kb[b, h][:].rearrange("p a x -> p (a x)")
             )
 
-        def interleave_q(b, h):
-            qt = work.tile([P, 2048], BF16, name="qb", bufs=2, align_bytes=64)
-            qb[b, h] = qt
-            nc.vector.tensor_copy(
-                out=qt[:].rearrange("p (c i t) -> p c i t", i=8, t=4),
-                in_=qp[b, h][:].rearrange("p a c t i -> p (a c) i t"),
-            )
+        def interleave_q(b, h, part, engine):
+            if part == 0:
+                qt = work.tile([P, 64, 8, 4], BF16, name="qb", bufs=2, align_bytes=64)
+                qb[b, h] = qt
+            if engine == "v":
+                nc.vector.tensor_copy(
+                    out=qb[b, h][:],
+                    in_=qp[b, h][:].rearrange("p a c t i -> p (a c) i t"),
+                )
+            else:
+                cs = slice(part * 16, (part + 1) * 16)
+                nc.gpsimd.tensor_scalar(
+                    out=qb[b, h][:, cs],
+                    in0=qp[b, h][:].rearrange("p a c t i -> p (a c) i t")[:, cs],
+                    scalar1=1.0,
+                    scalar2=1.0,
+                    op0=ALU.mult,
+                    op1=ALU.mult,
+                )
 
         def quant_q(b, h):
             cols = slice(h * 512, (h + 1) * 512)
-            nc.vector.quantize_mx(out=qc[b][:, cols].bitcast(FP8X4), scales=qs[b][:, cols], in_=qb[b, h][:])
+            nc.vector.quantize_mx(out=qc[b][:, cols].bitcast(FP8X4), scales=qs[b][:, cols], in_=qb[b, h][:].rearrange("p c i t -> p (c i t)"))
 
         vb = {}
 
         vt_bank = {}
 
         def v_turn(b, h, e4):
-            bank = ps.tile([P, 256, 4], BF16, name="tr", bufs=2)
+            bank = ps.tile([P, 256, 4], BF16, name="tr", bufs=3)
             vt_bank[b, h, e4] = bank
             for i in range(2):
                 e0 = e4 * 256 + i * 128
                 nc.tensor.matmul(
-                    bank[:, i * 128 : (i + 1) * 128, :],
+                    bank[:, i * 128 : (i + 1) * 128, :].rearrange("p (c i) t -> p c t i", i=8),
                     lhsT=identb[:],
-                    rhs=v_sb[b, h][:, :, e0 : e0 + 128].rearrange("p t e -> p e t"),
+                    rhs=v_sb[b, h][:, :, e0 : e0 + 128].rearrange("p t (c i) -> p c t i", i=8),
                     start=True,
                     stop=True,
                 )
 
         def v_copy(b, h, e4):
-            if e4 % 2 == 0:
+            if (b, h, e4 // 2) not in vb:
                 vt = work.tile([P, 2, 1024], BF16, name="vb", bufs=2, align_bytes=64)
                 vb[b, h, e4 // 2] = vt
             nc.vector.tensor_tensor(
@@ -197,7 +228,7 @@ def tile_gatedattentionunitsquaredrelu_x1_kernel(tc, z, gq, cq, gk, g, v, u, out
 
         def scores(k, hh, tk):
             b, h = divmod(k, 2)
-            bank = ps.tile([P, 512], F32, name="st", bufs=4)
+            bank = ps.tile([P, 512], F32, name="st", bufs=3)
             sc[k, hh, tk] = bank
             kcols = slice(hh * 512 + tk * P, hh * 512 + (tk + 1) * P)
             qcols = slice(h * 512, (h + 1) * 512)
@@ -212,7 +243,7 @@ def tile_gatedattentionunitsquaredrelu_x1_kernel(tc, z, gq, cq, gk, g, v, u, out
             )
 
         def relu_root(k, hh, tk, engine):
-            if (hh, tk) == (0, 0):
+            if k not in xr:
                 xt = work.tile([P, 4, 2, 32, 4, 4], F32, name="xt", bufs=2)
                 xr[k] = xt
             j = hh * 4 + tk
@@ -223,70 +254,78 @@ def tile_gatedattentionunitsquaredrelu_x1_kernel(tc, z, gq, cq, gk, g, v, u, out
             else:
                 nc.vector.tensor_scalar(out=dst, in0=src, scalar1=rs[:, j : j + 1], scalar2=0.0, op0=ALU.mult, op1=ALU.max)
 
-        def square(n, engine):
-            k, a = divmod(n, 4)
-            pt = work.tile([P, 2, 512], BF16, name="pb", bufs=3, align_bytes=64)
-            pb[n] = pt
-            dst = pt[:].rearrange("p h (c i t) -> p (h c) t i", i=4, t=4)
-            src = xr[k][:, a].rearrange("p h c t i -> p (h c) t i")
+        def square(m, engine):
+            k, a = divmod(2 * m, 4)
+            pt = work.tile([P, 2, 2, 512], BF16, name="pb", bufs=2, align_bytes=64)
+            pb[m] = pt
+            dst = pt[:].rearrange("p a h (c i t) -> p (a h c) t i", i=4, t=4)
+            src = xr[k][:, a : a + 2].rearrange("p a h c t i -> p (a h c) t i")
             if engine == "s":
                 nc.scalar.activation(out=dst, in_=src, func=ACT.Square)
             else:
                 nc.vector.tensor_tensor(out=dst, in0=src, in1=src, op=ALU.mult)
 
-        def quant_p(n):
-            ct = work.tile([P, 256], U32, name="pc", bufs=3, align_bytes=64)
-            pc[n] = ct
-            sct = work.tile([P, 256], U8, name="psc", bufs=3, align_bytes=64)
-            psc[n] = sct
-            nc.vector.quantize_mx(out=ct[:].bitcast(FP8X4), scales=sct[:], in_=pb[n][:].rearrange("p h x -> p (h x)"))
+        def quant_p(m):
+            ct = work.tile([P, 512], U32, name="pc", bufs=2, align_bytes=64)
+            pc[m] = ct
+            sct = work.tile([P, 512], U8, name="psc", bufs=2, align_bytes=64)
+            psc[m] = sct
+            nc.vector.quantize_mx(out=ct[:].bitcast(FP8X4), scales=sct[:], in_=pb[m][:].rearrange("p a h x -> p (a h x)"))
 
         def st2(n, e):
             b, h, t, cols = where(n)
             bank = ps.tile([P, 512], F32, name="cb", bufs=2)
             cb[n, e] = bank
             for hh in range(2):
-                pcols = slice(hh * P, (hh + 1) * P)
+                pcols = slice((n % 2 * 2 + hh) * P, (n % 2 * 2 + hh + 1) * P)
                 ecols = slice(e * 512, (e + 1) * 512)
                 nc.tensor.matmul_mx(
                     out=bank[:],
-                    lhsT=pc[n][:, pcols].bitcast(FP8X4),
-                    lhsT_scale=psc[n][:, pcols],
+                    lhsT=pc[n // 2][:, pcols].bitcast(FP8X4),
+                    lhsT_scale=psc[n // 2][:, pcols],
                     rhs=vc[b, hh][:, ecols].bitcast(FP8X4),
                     rhs_scale=vs[b, hh][:, ecols],
                     start=(hh == 0),
                     stop=(hh == 1),
                 )
 
-        def silu(n):
-            b, h, t, cols = where(n)
-            gt = work.tile([P, E], F32, name="gate", bufs=3)
-            gate[n] = gt
-            nc.scalar.activation(out=gt[:], in_=u_sb[b, h][:, t, :], func=ACT.Silu)
+        def silu(m):
+            b, h, t, cols = where(2 * m)
+            gt = work.tile([P, 2, E], F32, name="gate", bufs=2)
+            gate[m] = gt
+            nc.scalar.activation(
+                out=gt[:].rearrange("p a e -> p (a e)"),
+                in_=u_sb[b, h][:, t : t + 2, :].rearrange("p a e -> p (a e)"),
+                func=ACT.Silu,
+            )
 
         def apply_gate(n, e):
-            if e == 0:
+            if n not in o32:
                 ot = work.tile([P, E], F32, name="o32", bufs=4)
                 o32[n] = ot
             ecols = slice(e * 512, (e + 1) * 512)
-            nc.vector.tensor_tensor(out=o32[n][:, ecols], in0=cb[n, e][:], in1=gate[n][:, ecols], op=ALU.mult)
+            nc.vector.tensor_tensor(out=o32[n][:, ecols], in0=cb[n, e][:], in1=gate[n // 2][:, n % 2, ecols], op=ALU.mult)
 
         def store_out(n):
             b, h, t, cols = where(n)
             dst = out_0[b, h * 512 : (h + 1) * 512, :].rearrange("(m t) e -> m t e", t=4)[:, t, :]
             nc.sync.dma_start(out=dst, in_=o32[n][:])
 
-        def round_out(n):
-            obt = work.tile([P, E], BF16, name="ob", bufs=3)
-            ob[n] = obt
-            nc.vector.tensor_copy(out=obt[:], in_=o32[n][:])
+        def round_out(n, lo, hi, engine):
+            if n not in ob:
+                obt = work.tile([P, E], BF16, name="ob", bufs=3)
+                ob[n] = obt
+            part = slice(lo, hi)
+            if engine == "g":
+                nc.gpsimd.tensor_scalar(
+                    out=ob[n][:, part], in0=o32[n][:, part], scalar1=1.0, scalar2=1.0, op0=ALU.mult, op1=ALU.mult
+                )
+            else:
+                nc.vector.tensor_copy(out=ob[n][:, part], in_=o32[n][:, part])
 
         def turn(n, grp):
             b, h, t, cols = where(n)
-            if t == 1:
-                grt = work.tile([P, 2048], BF16, name="gr", bufs=3, align_bytes=64)
-                gr[n // 4, grp] = grt
-            bank = ps.tile([P, 2, 2, P], F32, name="tr", bufs=2)
+            bank = ps.tile([P, 2, 2, P], F32, name="tr", bufs=3)
             for a in range(2):
                 words = ob[n - 1 + a][:].bitcast(F32)
                 for w in range(2):
@@ -295,23 +334,28 @@ def tile_gatedattentionunitsquaredrelu_x1_kernel(tc, z, gq, cq, gk, g, v, u, out
 
         def turn_copy(n, grp):
             b, h, t, cols = where(n)
+            if (n // 4, grp) not in gr:
+                grt = work.tile([P, 2048], BF16, name="gr", bufs=3, align_bytes=64)
+                gr[n // 4, grp] = grt
             dst = gr[n // 4, grp][:].bitcast(F32).rearrange("p (m x) -> p m x", x=8)[:, :, 2 * (t - 1) : 2 * (t - 1) + 4]
             nc.scalar.copy(out=dst, in_=turned[n, grp][:].rearrange("p a w m -> p m (a w)"))
 
         def quant_out(k, grp):
-            if grp == 0:
+            if k not in oc:
                 oct_ = work.tile([P, 2, 512], U32, name="oc", bufs=2, align_bytes=64)
                 oc[k] = oct_
                 ost = work.tile([P, 2, 512], U8, name="osc", bufs=2, align_bytes=64)
                 osc[k] = ost
             nc.vector.quantize_mx(out=oc[k][:, grp, :].bitcast(FP8X4), scales=osc[k][:, grp, :], in_=gr[k, grp][:])
 
-        def store_planes(k):
+        def store_words(k, grp):
             tok = slice(k * 512, (k + 1) * 512)
-            for grp in range(2):
-                nc.sync.dma_start(
-                    out=out_1[grp, :, tok, :].rearrange("p m t -> p (m t)").bitcast(I32), in_=oc[k][:, grp, :].bitcast(I32)
-                )
+            nc.sync.dma_start(
+                out=out_1[grp, :, tok, :].rearrange("p m t -> p (m t)").bitcast(I32), in_=oc[k][:, grp, :].bitcast(I32)
+            )
+
+        def store_scales(k):
+            tok = slice(k * 512, (k + 1) * 512)
             for Q in range(4):
                 nc.sync.dma_start(
                     out=out_2[:, 4 * Q : 4 * Q + 4, tok].rearrange("g q m -> q g m").bitcast(I32),
@@ -319,334 +363,330 @@ def tile_gatedattentionunitsquaredrelu_x1_kernel(tc, z, gq, cq, gk, g, v, u, out
                 )
 
         with tc.manual_schedule():
-            load_rows(u_sb, u, "u", 1, 0)
             z_turn(0, 0)
             z_turn(0, 1)
-            q_make(0, 0)
+            load_z(1, 1, 1)
+            load_rows(u_sb, u, "u", 0, 1)
+            load_rows(v_sb, v, "v", 1, 0)
             k_make(0, 0)
             z_turn(0, 2)
             k_make(0, 1)
-            z_turn(0, 3)
             k_make(0, 2)
+            q_make(0, 0)
+            z_turn(0, 3)
             q_make(0, 1)
             k_make(0, 3)
-            quant_k(0, 0)
-            v_turn(0, 0, 0)
             q_make(0, 2)
-            interleave_q(0, 0)
-            v_turn(0, 0, 1)
             q_make(0, 3)
+            interleave_q(0, 0, 0, "v")
             quant_k(0, 1)
             quant_q(0, 0)
-            interleave_q(0, 1)
-            scores(0, 0, 0)
-            scores(0, 0, 1)
-            relu_root(0, 0, 0, "s")
-            scores(0, 0, 2)
-            scores(0, 0, 3)
-            v_copy(0, 0, 0)
-            relu_root(0, 0, 1, "s")
-            scores(0, 1, 0)
+            quant_k(0, 0)
+            interleave_q(0, 1, 0, "v")
             quant_q(0, 1)
-            relu_root(0, 0, 2, "s")
-            v_turn(0, 1, 0)
-            v_copy(0, 0, 1)
-            relu_root(0, 0, 3, "s")
-            relu_root(0, 1, 0, "s")
-            scores(0, 1, 1)
-            quant_v(0, 0, 0)
-            scores(0, 1, 2)
-            silu(0)
-            v_copy(0, 1, 0)
+            v_turn(0, 0, 0)
+            v_copy(0, 0, 0)
+            v_turn(0, 0, 1)
             scores(0, 1, 3)
-            scores(1, 0, 0)
-            v_turn(0, 1, 1)
-            relu_root(0, 1, 1, "s")
-            relu_root(0, 1, 2, "s")
-            v_turn(0, 0, 2)
-            v_copy(0, 1, 1)
             relu_root(0, 1, 3, "s")
-            relu_root(1, 0, 0, "s")
-            quant_v(0, 1, 0)
-            v_turn(0, 0, 3)
-            square(0, "s")
+            scores(0, 1, 2)
+            v_copy(0, 0, 1)
+            v_turn(0, 1, 0)
+            scores(0, 1, 1)
+            relu_root(0, 1, 2, "s")
+            scores(0, 1, 0)
+            relu_root(0, 1, 1, "s")
+            scores(0, 0, 3)
+            v_copy(0, 1, 0)
+            v_turn(0, 1, 1)
+            relu_root(0, 1, 0, "s")
+            scores(0, 0, 2)
+            scores(0, 0, 1)
+            relu_root(0, 0, 3, "s")
+            scores(0, 0, 0)
+            relu_root(0, 0, 2, "s")
+            v_copy(0, 1, 1)
+            v_turn(0, 0, 2)
+            relu_root(0, 0, 1, "s")
+            relu_root(0, 0, 0, "s")
+            quant_v(0, 0, 0)
             v_copy(0, 0, 2)
-            z_turn(1, 0)
-            v_copy(0, 0, 3)
+            v_turn(0, 0, 3)
             load_rows(v_sb, v, "v", 1, 1)
-            square(1, "s")
+            load_rows(u_sb, u, "u", 1, 0)
+            quant_v(0, 1, 0)
             v_turn(0, 1, 2)
-            quant_p(0)
-            quant_v(0, 0, 1)
-            q_make(1, 0)
-            k_make(1, 0)
+            v_copy(0, 0, 3)
+            square(0, "s")
             v_turn(0, 1, 3)
             v_copy(0, 1, 2)
-            scores(1, 0, 1)
-            quant_p(1)
-            silu(1)
+            quant_v(0, 0, 1)
+            z_turn(1, 0)
             v_copy(0, 1, 3)
+            quant_v(0, 1, 1)
+            silu(0)
+            zq_turn(1, 0, 0)
+            scores(1, 0, 0)
+            relu_root(1, 0, 0, "s")
+            q_plane(1, 0, 0)
+            scores(1, 0, 1)
+            k_make(1, 0)
+            zq_turn(1, 0, 1)
+            relu_root(1, 0, 1, "s")
+            q_plane(1, 0, 1)
             z_turn(1, 1)
             scores(1, 0, 2)
-            quant_v(0, 1, 1)
-            relu_root(1, 0, 1, "s")
-            z_turn(1, 2)
-            q_make(1, 1)
-            k_make(1, 1)
+            square(1, "s")
+            relu_root(1, 0, 2, "s")
+            q_plane(1, 0, 2)
+            quant_p(0)
             scores(1, 0, 3)
-            k_make(1, 2)
+            zq_turn(1, 1, 0)
+            relu_root(1, 0, 3, "s")
+            q_plane(1, 0, 3)
+            k_make(1, 1)
+            interleave_q(1, 0, 0, "v")
+            scores(1, 1, 0)
             st2(0, 0)
             st2(0, 1)
             quant_k(1, 0)
-            q_make(1, 2)
-            scores(1, 1, 0)
-            interleave_q(1, 0)
-            v_turn(1, 0, 0)
-            relu_root(1, 0, 2, "s")
-            apply_gate(0, 0)
-            scores(1, 1, 1)
-            relu_root(1, 0, 3, "s")
-            z_turn(1, 3)
-            apply_gate(0, 1)
-            square(2, "s")
-            st2(1, 0)
-            v_copy(1, 0, 0)
-            store_out(0)
-            st2(1, 1)
-            round_out(0)
-            q_make(1, 3)
-            scores(1, 1, 2)
-            k_make(1, 3)
-            v_turn(1, 0, 1)
-            quant_p(2)
             relu_root(1, 1, 0, "s")
-            apply_gate(1, 0)
-            relu_root(1, 1, 1, "s")
-            interleave_q(1, 1)
-            scores(1, 1, 3)
-            st2(2, 0)
-            silu(2)
-            apply_gate(1, 1)
-            square(3, "s")
-            quant_q(1, 0)
-            store_out(1)
-            st2(2, 1)
-            round_out(1)
-            relu_root(1, 1, 2, "s")
-            scores(2, 0, 0)
-            scores(2, 0, 1)
-            v_copy(1, 0, 1)
-            relu_root(1, 1, 3, "s")
-            turn(1, 0)
-            quant_q(1, 1)
-            silu(3)
-            v_turn(1, 1, 0)
-            quant_v(1, 0, 0)
-            quant_p(3)
-            square(4, "s")
+            z_turn(1, 2)
+            q_plane(1, 1, 0)
+            silu(1)
             load_rows(u_sb, u, "u", 1, 1)
-            scores(2, 0, 2)
-            apply_gate(2, 0)
-            scores(2, 0, 3)
-            apply_gate(2, 1)
-            st2(3, 0)
-            turn_copy(1, 0)
-            v_copy(1, 1, 0)
-            store_out(2)
-            st2(3, 1)
+            zq_turn(1, 1, 1)
+            scores(1, 1, 1)
+            relu_root(1, 1, 1, "s")
+            q_plane(1, 1, 1)
+            apply_gate(0, 0)
+            apply_gate(0, 1)
+            store_out(0)
+            k_make(1, 2)
+            scores(1, 1, 2)
+            relu_root(1, 1, 2, "s")
+            q_plane(1, 1, 2)
+            st2(1, 0)
+            st2(1, 1)
+            scores(1, 1, 3)
+            z_turn(1, 3)
+            quant_q(1, 0)
+            relu_root(1, 1, 3, "s")
+            square(2, "s")
+            q_plane(1, 1, 3)
+            v_turn(1, 0, 0)
+            scores(2, 0, 0)
+            quant_p(1)
+            k_make(1, 3)
+            apply_gate(1, 0)
+            apply_gate(1, 1)
+            store_out(1)
             relu_root(2, 0, 0, "s")
-            round_out(2)
-            turn(1, 1)
-            silu(4)
-            quant_p(4)
-            v_turn(1, 1, 1)
-            apply_gate(3, 0)
+            scores(2, 0, 1)
+            interleave_q(1, 1, 0, "v")
+            st2(2, 0)
+            st2(2, 1)
             relu_root(2, 0, 1, "s")
-            apply_gate(3, 1)
+            v_turn(1, 0, 1)
+            scores(2, 0, 2)
+            silu(2)
+            v_copy(1, 0, 0)
+            quant_q(1, 1)
+            quant_k(1, 1)
             relu_root(2, 0, 2, "s")
-            st2(4, 0)
-            square(5, "v")
+            scores(2, 0, 3)
+            apply_gate(2, 0)
+            apply_gate(2, 1)
+            store_out(2)
+            v_turn(1, 1, 0)
+            relu_root(2, 0, 3, "s")
+            v_copy(1, 0, 1)
+            scores(2, 1, 0)
+            st2(3, 0)
+            st2(3, 1)
+            relu_root(2, 1, 0, "s")
+            square(3, "s")
+            scores(2, 1, 1)
+            v_turn(1, 1, 1)
+            quant_p(2)
+            v_copy(1, 1, 0)
+            apply_gate(3, 0)
+            relu_root(2, 1, 1, "s")
+            apply_gate(3, 1)
             store_out(3)
-            turn_copy(1, 1)
+            scores(2, 1, 2)
+            quant_v(1, 0, 0)
+            st2(4, 0)
             st2(4, 1)
-            silu(5)
-            round_out(3)
+            relu_root(2, 1, 2, "s")
+            scores(2, 1, 3)
             v_turn(1, 0, 2)
             v_copy(1, 1, 1)
-            relu_root(2, 0, 3, "s")
-            quant_k(1, 1)
-            v_turn(1, 0, 3)
-            square(6, "s")
-            quant_v(1, 1, 0)
-            quant_p(5)
-            scores(2, 1, 0)
-            v_copy(1, 0, 2)
-            silu(6)
-            scores(2, 1, 1)
-            scores(2, 1, 2)
-            apply_gate(4, 0)
-            scores(2, 1, 3)
-            turn(3, 0)
-            relu_root(2, 1, 0, "s")
-            apply_gate(4, 1)
-            st2(5, 0)
-            relu_root(2, 1, 1, "s")
-            quant_p(6)
-            store_out(4)
-            round_out(4)
-            st2(5, 1)
-            turn_copy(3, 0)
-            v_copy(1, 0, 3)
-            scores(3, 0, 0)
-            square(7, "s")
-            scores(3, 0, 1)
-            apply_gate(5, 0)
-            turn(3, 1)
-            quant_v(1, 0, 1)
-            v_turn(1, 1, 2)
-            relu_root(2, 1, 2, "s")
-            apply_gate(5, 1)
+            round_out(0, 0, 1024, "v")
+            silu(3)
             relu_root(2, 1, 3, "s")
-            quant_p(7)
-            st2(6, 0)
-            turn_copy(3, 1)
-            store_out(5)
-            round_out(5)
-            st2(6, 1)
-            silu(7)
-            v_copy(1, 1, 2)
-            turn(5, 0)
-            apply_gate(6, 0)
-            square(8, "s")
-            v_turn(1, 1, 3)
-            apply_gate(6, 1)
-            square(9, "v")
-            store_out(6)
-            turn_copy(5, 0)
-            st2(7, 0)
+            scores(3, 0, 0)
+            apply_gate(4, 0)
+            apply_gate(4, 1)
+            store_out(4)
             relu_root(3, 0, 0, "s")
-            st2(7, 1)
-            round_out(6)
-            silu(8)
+            scores(3, 0, 1)
+            v_copy(1, 0, 2)
+            v_turn(1, 0, 3)
+            st2(5, 0)
+            st2(5, 1)
+            round_out(1, 0, 1024, "v")
+            quant_v(1, 1, 0)
             scores(3, 0, 2)
-            quant_p(8)
-            scores(3, 0, 3)
-            v_copy(1, 1, 3)
-            scores(3, 1, 0)
             relu_root(3, 0, 1, "s")
-            apply_gate(7, 0)
-            turn(5, 1)
+            square(4, "s")
+            v_copy(1, 0, 3)
+            quant_p(3)
+            scores(3, 0, 3)
+            turn(1, 0)
             relu_root(3, 0, 2, "s")
-            quant_v(1, 1, 1)
-            st2(8, 0)
-            silu(9)
-            apply_gate(7, 1)
-            scores(3, 1, 1)
-            quant_p(9)
-            scores(3, 1, 2)
-            store_out(7)
-            st2(8, 1)
-            round_out(7)
+            v_turn(1, 1, 2)
+            turn_copy(1, 0)
+            apply_gate(5, 0)
+            apply_gate(5, 1)
+            store_out(5)
+            turn(1, 1)
+            round_out(2, 0, 1024, "v")
+            st2(6, 0)
+            scores(3, 1, 0)
+            st2(6, 1)
             relu_root(3, 0, 3, "s")
-            apply_gate(8, 0)
-            square(10, "s")
-            turn(7, 0)
-            apply_gate(8, 1)
-            st2(9, 0)
-            quant_out(0, 0)
+            v_copy(1, 1, 2)
+            v_turn(1, 1, 3)
+            scores(3, 1, 1)
+            silu(4)
+            quant_v(1, 0, 1)
             relu_root(3, 1, 0, "s")
-            store_out(8)
-            st2(9, 1)
-            round_out(8)
-            turn_copy(7, 0)
-            scores(3, 1, 3)
-            quant_p(10)
-            turn_copy(5, 1)
-            apply_gate(9, 0)
+            turn_copy(1, 1)
+            apply_gate(6, 0)
+            apply_gate(6, 1)
+            store_out(6)
+            round_out(3, 0, 1024, "v")
+            scores(3, 1, 2)
             relu_root(3, 1, 1, "s")
-            turn(7, 1)
-            apply_gate(9, 1)
-            silu(10)
-            st2(10, 0)
-            quant_out(0, 1)
-            store_out(9)
-            st2(10, 1)
-            round_out(9)
-            square(11, "s")
-            store_planes(0)
-            apply_gate(10, 0)
-            turn(9, 0)
-            apply_gate(10, 1)
+            v_copy(1, 1, 3)
+            st2(7, 0)
+            st2(7, 1)
+            scores(3, 1, 3)
             relu_root(3, 1, 2, "s")
-            quant_p(11)
+            turn(3, 0)
+            square(5, "s")
+            turn_copy(3, 0)
+            turn(3, 1)
+            round_out(4, 0, 1024, "v")
             relu_root(3, 1, 3, "s")
+            quant_p(4)
+            quant_v(1, 1, 1)
+            apply_gate(7, 0)
+            apply_gate(7, 1)
+            store_out(7)
+            st2(8, 0)
+            st2(8, 1)
+            turn_copy(3, 1)
+            round_out(5, 0, 1024, "v")
+            silu(5)
+            apply_gate(8, 0)
+            apply_gate(8, 1)
+            store_out(8)
+            st2(9, 0)
+            turn(5, 0)
+            st2(9, 1)
+            turn(5, 1)
+            round_out(6, 0, 1024, "v")
+            turn_copy(5, 0)
+            square(6, "s")
+            quant_p(5)
+            apply_gate(9, 0)
+            apply_gate(9, 1)
+            store_out(9)
+            quant_out(0, 0)
+            store_words(0, 0)
+            st2(10, 0)
+            st2(10, 1)
+            round_out(7, 0, 1024, "v")
+            turn_copy(5, 1)
+            silu(6)
+            turn(7, 0)
+            apply_gate(10, 0)
+            apply_gate(10, 1)
             store_out(10)
-            round_out(10)
+            round_out(8, 0, 1024, "v")
+            turn(7, 1)
             st2(11, 0)
-            turn_copy(7, 1)
-            square(13, "v")
             st2(11, 1)
-            silu(11)
-            turn(9, 1)
-            quant_out(1, 0)
-            square(12, "s")
+            turn_copy(7, 0)
+            square(7, "s")
+            quant_out(0, 1)
+            store_words(0, 1)
+            store_scales(0)
+            round_out(9, 0, 1024, "v")
+            quant_p(6)
             apply_gate(11, 0)
             apply_gate(11, 1)
-            turn_copy(9, 0)
-            quant_p(12)
             store_out(11)
-            round_out(11)
-            silu(12)
+            turn_copy(7, 1)
             st2(12, 0)
-            quant_p(13)
             st2(12, 1)
-            quant_out(1, 1)
-            turn_copy(9, 1)
-            turn(11, 0)
+            turn(9, 0)
+            round_out(10, 0, 1024, "v")
+            turn(9, 1)
+            silu(7)
             apply_gate(12, 0)
-            silu(13)
-            store_planes(1)
-            turn(11, 1)
             apply_gate(12, 1)
-            st2(13, 0)
-            square(14, "s")
-            round_out(12)
             store_out(12)
+            quant_out(1, 0)
+            store_words(1, 0)
+            st2(13, 0)
             st2(13, 1)
+            turn_copy(9, 0)
+            round_out(11, 0, 1024, "v")
             apply_gate(13, 0)
-            turn_copy(11, 0)
-            quant_p(14)
+            quant_p(7)
             apply_gate(13, 1)
-            silu(14)
-            st2(14, 0)
-            quant_out(2, 0)
             store_out(13)
+            turn_copy(9, 1)
+            st2(14, 0)
             st2(14, 1)
-            square(15, "s")
-            round_out(13)
+            turn(11, 0)
+            round_out(12, 0, 1024, "v")
+            turn(11, 1)
+            quant_out(1, 1)
+            store_words(1, 1)
+            store_scales(1)
             apply_gate(14, 0)
-            turn(13, 0)
-            turn_copy(11, 1)
             apply_gate(14, 1)
-            silu(15)
-            quant_p(15)
-            turn(13, 1)
             store_out(14)
-            round_out(14)
+            turn_copy(11, 0)
+            round_out(13, 0, 1024, "v")
             st2(15, 0)
-            quant_out(2, 1)
-            turn_copy(13, 0)
             st2(15, 1)
+            turn_copy(11, 1)
+            turn(13, 0)
+            round_out(14, 0, 1024, "v")
             apply_gate(15, 0)
-            turn_copy(13, 1)
-            store_planes(2)
             apply_gate(15, 1)
-            round_out(15)
             store_out(15)
+            turn(13, 1)
+            quant_out(2, 0)
+            store_words(2, 0)
+            round_out(15, 0, 512, "v")
+            turn_copy(13, 0)
+            round_out(15, 512, 1024, "v")
             turn(15, 0)
+            turn_copy(13, 1)
             turn(15, 1)
+            quant_out(2, 1)
+            store_words(2, 1)
+            store_scales(2)
             turn_copy(15, 0)
             turn_copy(15, 1)
             quant_out(3, 0)
+            store_words(3, 0)
             quant_out(3, 1)
-            store_planes(3)
+            store_words(3, 1)
+            store_scales(3)

from contextlib import ExitStack

import concourse.mybir as mybir
from concourse.masks import make_identity

B, S, Z, E = 2, 1024, 512, 1024
P = 128
FLOPS = 2 * B * S * S * (Z + E)

F32 = mybir.dt.float32
BF16 = mybir.dt.bfloat16
U32 = mybir.dt.uint32
I32 = mybir.dt.int32
U8 = mybir.dt.uint8
FP8X4 = mybir.dt.float8_e4m3fn_x4
ACT = mybir.ActivationFunctionType
ALU = mybir.AluOpType


def tile_gatedattentionunitsquaredrelu_x1_kernel(tc, z, gq, cq, gk, g, v, u, out_0, out_1, out_2):
    nc = tc.nc
    with ExitStack() as ctx:
        const = ctx.enter_context(tc.tile_pool(name="const", bufs=1))
        work = ctx.enter_context(tc.tile_pool(name="work", bufs=2))
        ps = ctx.enter_context(tc.psum_pool(name="ps", bufs=2))

        gq_raw = const.tile([P, 4], BF16, name="gq_raw")
        cq_raw = const.tile([P, 4], BF16, name="cq_raw")
        gk_raw = const.tile([P, 4], BF16, name="gk_raw")
        g_raw = const.tile([P, 2, 4], BF16, name="g_raw")
        nc.scalar.dma_start(out=gk_raw[:], in_=gk.rearrange("(p t) -> p t", t=4))
        nc.scalar.dma_start(out=gq_raw[:], in_=gq.rearrange("(p t) -> p t", t=4))
        nc.scalar.dma_start(out=cq_raw[:], in_=cq.rearrange("(p t) -> p t", t=4))
        nc.scalar.dma_start(out=g_raw[:], in_=g.rearrange("(h p t) -> p h t", h=2, t=4))

        z_sb, v_sb, u_sb = {}, {}, {}

        def load_z(b, h, parts):
            z_sb[b, h] = const.tile([P, 4, Z], BF16, name="z", bufs=3)
            src = z[b, h * 512 : (h + 1) * 512, :].rearrange("(m t) c -> m t c", t=4)
            w = 4 // parts
            for i in range(parts):
                nc.sync.dma_start(out=z_sb[b, h][:, i * w : (i + 1) * w, :], in_=src[:, i * w : (i + 1) * w, :])

        def load_rows(store, src, name, b, h):
            store[b, h] = const.tile([P, 4, E], BF16, name=name, bufs=3)
            nc.sync.dma_start(out=store[b, h][:], in_=src[b, h * 512 : (h + 1) * 512, :].rearrange("(m t) e -> m t e", t=4))

        load_z(0, 0, 2)
        load_z(0, 1, 2)
        load_rows(v_sb, v, "v", 0, 0)
        load_rows(v_sb, v, "v", 0, 1)
        load_rows(u_sb, u, "u", 0, 0)
        load_z(1, 0, 1)

        warm = const.tile([P, 1], F32, name="warm")
        nc.vector.memset(warm[:], 0.0)
        warm2 = const.tile([P, 1], F32, name="warm2")
        nc.scalar.activation(out=warm2[:], in_=warm[:], func=ACT.Silu)
        ident = const.tile([P, P], F32, name="ident")
        make_identity(nc, ident[:])
        gq32 = const.tile([P, 4], F32, name="gq32")
        cq32 = const.tile([P, 4], F32, name="cq32")
        gf = g_raw[:].rearrange("p h t -> p (h t)")
        neg = const.tile([P, 8], F32, name="neg")
        mag = const.tile([P, 8], F32, name="mag")
        half = const.tile([P, 8], F32, name="half")
        root = const.tile([P, 8], F32, name="root")
        rs = const.tile([P, 8], F32, name="rs")
        step = const.tile([P, 8], F32, name="step")
        sgn = const.tile([P, 8], F32, name="sgn")
        nc.gpsimd.memset(half[:], 0.5)
        nc.vector.tensor_copy(out=gq32[:], in_=gq_raw[:])
        nc.vector.tensor_copy(out=cq32[:], in_=cq_raw[:])
        nc.vector.tensor_scalar(out=neg[:], in0=gf, scalar1=-1.0, scalar2=None, op0=ALU.mult)
        nc.vector.tensor_scalar(out=step[:], in0=gf, scalar1=0.0, scalar2=2.0, op0=ALU.is_ge, op1=ALU.mult)
        nc.vector.tensor_tensor(out=mag[:], in0=neg[:], in1=gf, op=ALU.max)
        nc.vector.tensor_scalar(out=sgn[:], in0=step[:], scalar1=-1.0, scalar2=None, op0=ALU.add)
        nc.gpsimd.tensor_tensor(out=root[:], in0=mag[:], in1=half[:], op=ALU.pow)
        nc.gpsimd.tensor_scalar(out=rs[:], in0=root[:], scalar1=1.0 / 64.0, scalar2=0.0, op0=ALU.mult, op1=ALU.add)
        sgnb = const.tile([P, 4 * 2], BF16, name="sgnb")
        nc.vector.tensor_copy(out=sgnb[:], in_=sgn[:])
        identb = const.tile([P, P], BF16, name="identb")
        nc.vector.tensor_copy(out=identb[:], in_=ident[:])

        kc, ks, qc, qs, vc, vs = {}, {}, {}, {}, {}, {}
        for b in range(B):
            kc[b] = const.tile([P, S], U32, name="kc%d" % b, align_bytes=64)
            ks[b] = const.tile([P, S], U8, name="ks%d" % b, align_bytes=64)
            qc[b] = const.tile([P, S], U32, name="qc%d" % b, align_bytes=64)
            qs[b] = const.tile([P, S], U8, name="qs%d" % b, align_bytes=64)
            for h in range(2):
                vc[b, h] = const.tile([P, E], U32, name="vc%d%d" % (b, h), align_bytes=64)
                vs[b, h] = const.tile([P, E], U8, name="vs%d%d" % (b, h), align_bytes=64)

        kb, qp, qb = {}, {}, {}

        zt = {}

        def z_turn(b, zb):
            h, tp = divmod(zb, 2)
            bank = ps.tile([P, 2, 2, P], F32, name="st", bufs=3)
            words = z_sb[b, h][:].rearrange("p t c -> p (t c)").bitcast(F32)
            for a in range(2):
                t = 2 * tp + a
                for w in range(2):
                    nc.tensor.transpose(bank[:, w, a, :], words[:, 256 * t + w : 256 * (t + 1) : 2], ident[:])
            zt[b, zb] = bank[:].rearrange("p w a m -> p (w a m)").bitcast(BF16).rearrange("p (w i e) -> p w i e", w=2, e=2)

        def k_make(b, zb):
            h, tp = divmod(zb, 2)
            if (b, h) not in kb:
                kt = work.tile([P, 2, 1024], BF16, name="kb", bufs=2, align_bytes=64)
                kb[b, h] = kt
            nc.vector.tensor_tensor(
                out=kb[b, h][:, tp, :].rearrange("p (i w e) -> p i w e", w=2, e=2),
                in0=zt[b, zb].rearrange("p w i e -> p i w e"),
                in1=gk_raw[:].rearrange("p (w e) -> p w e", e=2).unsqueeze(1).to_broadcast([P, 256, 2, 2]),
                op=ALU.mult,
            )

        def q_make(b, zb):
            h, tp = divmod(zb, 2)
            if (b, h) not in qp:
                qt = work.tile([P, 2, 32, 4, 8], BF16, name="qp", bufs=2)
                qp[b, h] = qt
            for t in range(4):
                w, e = divmod(t, 2)
                nc.scalar.activation(
                    out=qp[b, h][:, tp, :, t, :],
                    in_=zt[b, zb][:, w, :, e].rearrange("p (c i) -> p c i", i=8),
                    func=ACT.Identity,
                    scale=gq32[:, t : t + 1],
                    bias=cq32[:, t : t + 1],
                )

        zp = {}

        def zq_turn(b, h, tp):
            bank = ps.tile([P, 2, 4, P], BF16, name="tr", bufs=3)
            zp[b, h, tp] = bank
            for i in range(2):
                for a in range(4):
                    nc.tensor.transpose(bank[:, i, a, :], z_sb[b, h][:, a, 2 * tp + i : Z : 4], identb[:])

        def q_plane(b, h, t):
            if (b, h) not in qp:
                qt = work.tile([P, 2, 32, 4, 8], BF16, name="qp", bufs=2)
                qp[b, h] = qt
            nc.vector.tensor_scalar(
                out=qp[b, h][:, :, :, t, :].rearrange("p a c i -> p (a c) i"),
                in0=zp[b, h, t // 2][:, t % 2].rearrange("p a m -> p (a m)").rearrange("p (c i) -> p c i", i=8),
                scalar1=gq32[:, t : t + 1],
                scalar2=cq32[:, t : t + 1],
                op0=ALU.mult,
                op1=ALU.add,
            )

        def quant_k(b, h):
            cols = slice(h * 512, (h + 1) * 512)
            nc.vector.quantize_mx(
                out=kc[b][:, cols].bitcast(FP8X4), scales=ks[b][:, cols], in_=kb[b, h][:].rearrange("p a x -> p (a x)")
            )

        def interleave_q(b, h, part, engine):
            if part == 0:
                qt = work.tile([P, 64, 8, 4], BF16, name="qb", bufs=2, align_bytes=64)
                qb[b, h] = qt
            if engine == "v":
                nc.vector.tensor_copy(
                    out=qb[b, h][:],
                    in_=qp[b, h][:].rearrange("p a c t i -> p (a c) i t"),
                )
            else:
                cs = slice(part * 16, (part + 1) * 16)
                nc.gpsimd.tensor_scalar(
                    out=qb[b, h][:, cs],
                    in0=qp[b, h][:].rearrange("p a c t i -> p (a c) i t")[:, cs],
                    scalar1=1.0,
                    scalar2=1.0,
                    op0=ALU.mult,
                    op1=ALU.mult,
                )

        def quant_q(b, h):
            cols = slice(h * 512, (h + 1) * 512)
            nc.vector.quantize_mx(out=qc[b][:, cols].bitcast(FP8X4), scales=qs[b][:, cols], in_=qb[b, h][:].rearrange("p c i t -> p (c i t)"))

        vb = {}

        vt_bank = {}

        def v_turn(b, h, e4):
            bank = ps.tile([P, 256, 4], BF16, name="tr", bufs=3)
            vt_bank[b, h, e4] = bank
            for i in range(2):
                e0 = e4 * 256 + i * 128
                nc.tensor.matmul(
                    bank[:, i * 128 : (i + 1) * 128, :].rearrange("p (c i) t -> p c t i", i=8),
                    lhsT=identb[:],
                    rhs=v_sb[b, h][:, :, e0 : e0 + 128].rearrange("p t (c i) -> p c t i", i=8),
                    start=True,
                    stop=True,
                )

        def v_copy(b, h, e4):
            if (b, h, e4 // 2) not in vb:
                vt = work.tile([P, 2, 1024], BF16, name="vb", bufs=2, align_bytes=64)
                vb[b, h, e4 // 2] = vt
            nc.vector.tensor_tensor(
                out=vb[b, h, e4 // 2][:, e4 % 2, :].rearrange("p (e t) -> p e t", t=4),
                in0=vt_bank[b, h, e4][:],
                in1=sgnb[:, h * 4 : (h + 1) * 4].unsqueeze(1).to_broadcast([P, 256, 4]),
                op=ALU.mult,
            )

        def quant_v(b, h, e2):
            cols = slice(e2 * 512, (e2 + 1) * 512)
            nc.vector.quantize_mx(out=vc[b, h][:, cols].bitcast(FP8X4), scales=vs[b, h][:, cols], in_=vb[b, h, e2][:].rearrange("p a x -> p (a x)"))

        def where(n):
            b, r = divmod(n, 8)
            h, t = divmod(r, 4)
            return b, h, t, slice(r * P, (r + 1) * P)

        turned, sc = {}, {}
        xr, pb, pc, psc, cb, gate, o32, ob, gr, oc, osc = {}, {}, {}, {}, {}, {}, {}, {}, {}, {}, {}

        def scores(k, hh, tk):
            b, h = divmod(k, 2)
            bank = ps.tile([P, 512], F32, name="st", bufs=3)
            sc[k, hh, tk] = bank
            kcols = slice(hh * 512 + tk * P, hh * 512 + (tk + 1) * P)
            qcols = slice(h * 512, (h + 1) * 512)
            nc.tensor.matmul_mx(
                out=bank[:],
                lhsT=kc[b][:, kcols].bitcast(FP8X4),
                lhsT_scale=ks[b][:, kcols],
                rhs=qc[b][:, qcols].bitcast(FP8X4),
                rhs_scale=qs[b][:, qcols],
                start=True,
                stop=True,
            )

        def relu_root(k, hh, tk, engine):
            if k not in xr:
                xt = work.tile([P, 4, 2, 32, 4, 4], F32, name="xt", bufs=2)
                xr[k] = xt
            j = hh * 4 + tk
            dst = xr[k][:, :, hh, :, tk, :]
            src = sc[k, hh, tk][:].rearrange("p (a c i) -> p a c i", a=4, i=4)
            if engine == "s":
                nc.scalar.activation(out=dst, in_=src, func=ACT.Relu, scale=rs[:, j : j + 1])
            else:
                nc.vector.tensor_scalar(out=dst, in0=src, scalar1=rs[:, j : j + 1], scalar2=0.0, op0=ALU.mult, op1=ALU.max)

        def square(m, engine):
            k, a = divmod(2 * m, 4)
            pt = work.tile([P, 2, 2, 512], BF16, name="pb", bufs=2, align_bytes=64)
            pb[m] = pt
            dst = pt[:].rearrange("p a h (c i t) -> p (a h c) t i", i=4, t=4)
            src = xr[k][:, a : a + 2].rearrange("p a h c t i -> p (a h c) t i")
            if engine == "s":
                nc.scalar.activation(out=dst, in_=src, func=ACT.Square)
            else:
                nc.vector.tensor_tensor(out=dst, in0=src, in1=src, op=ALU.mult)

        def quant_p(m):
            ct = work.tile([P, 512], U32, name="pc", bufs=2, align_bytes=64)
            pc[m] = ct
            sct = work.tile([P, 512], U8, name="psc", bufs=2, align_bytes=64)
            psc[m] = sct
            nc.vector.quantize_mx(out=ct[:].bitcast(FP8X4), scales=sct[:], in_=pb[m][:].rearrange("p a h x -> p (a h x)"))

        def st2(n, e):
            b, h, t, cols = where(n)
            bank = ps.tile([P, 512], F32, name="cb", bufs=2)
            cb[n, e] = bank
            for hh in range(2):
                pcols = slice((n % 2 * 2 + hh) * P, (n % 2 * 2 + hh + 1) * P)
                ecols = slice(e * 512, (e + 1) * 512)
                nc.tensor.matmul_mx(
                    out=bank[:],
                    lhsT=pc[n // 2][:, pcols].bitcast(FP8X4),
                    lhsT_scale=psc[n // 2][:, pcols],
                    rhs=vc[b, hh][:, ecols].bitcast(FP8X4),
                    rhs_scale=vs[b, hh][:, ecols],
                    start=(hh == 0),
                    stop=(hh == 1),
                )

        def silu(m):
            b, h, t, cols = where(2 * m)
            gt = work.tile([P, 2, E], F32, name="gate", bufs=2)
            gate[m] = gt
            nc.scalar.activation(
                out=gt[:].rearrange("p a e -> p (a e)"),
                in_=u_sb[b, h][:, t : t + 2, :].rearrange("p a e -> p (a e)"),
                func=ACT.Silu,
            )

        def apply_gate(n, e):
            if n not in o32:
                ot = work.tile([P, E], F32, name="o32", bufs=4)
                o32[n] = ot
            ecols = slice(e * 512, (e + 1) * 512)
            nc.vector.tensor_tensor(out=o32[n][:, ecols], in0=cb[n, e][:], in1=gate[n // 2][:, n % 2, ecols], op=ALU.mult)

        def store_out(n):
            b, h, t, cols = where(n)
            dst = out_0[b, h * 512 : (h + 1) * 512, :].rearrange("(m t) e -> m t e", t=4)[:, t, :]
            nc.sync.dma_start(out=dst, in_=o32[n][:])

        def round_out(n, lo, hi, engine):
            if n not in ob:
                obt = work.tile([P, E], BF16, name="ob", bufs=3)
                ob[n] = obt
            part = slice(lo, hi)
            if engine == "g":
                nc.gpsimd.tensor_scalar(
                    out=ob[n][:, part], in0=o32[n][:, part], scalar1=1.0, scalar2=1.0, op0=ALU.mult, op1=ALU.mult
                )
            else:
                nc.vector.tensor_copy(out=ob[n][:, part], in_=o32[n][:, part])

        def turn(n, grp):
            b, h, t, cols = where(n)
            bank = ps.tile([P, 2, 2, P], F32, name="tr", bufs=3)
            for a in range(2):
                words = ob[n - 1 + a][:].bitcast(F32)
                for w in range(2):
                    nc.tensor.transpose(bank[:, a, w, :], words[:, 256 * grp + w : 256 * (grp + 1) : 2], ident[:])
            turned[n, grp] = bank

        def turn_copy(n, grp):
            b, h, t, cols = where(n)
            if (n // 4, grp) not in gr:
                grt = work.tile([P, 2048], BF16, name="gr", bufs=3, align_bytes=64)
                gr[n // 4, grp] = grt
            dst = gr[n // 4, grp][:].bitcast(F32).rearrange("p (m x) -> p m x", x=8)[:, :, 2 * (t - 1) : 2 * (t - 1) + 4]
            nc.scalar.copy(out=dst, in_=turned[n, grp][:].rearrange("p a w m -> p m (a w)"))

        def quant_out(k, grp):
            if k not in oc:
                oct_ = work.tile([P, 2, 512], U32, name="oc", bufs=2, align_bytes=64)
                oc[k] = oct_
                ost = work.tile([P, 2, 512], U8, name="osc", bufs=2, align_bytes=64)
                osc[k] = ost
            nc.vector.quantize_mx(out=oc[k][:, grp, :].bitcast(FP8X4), scales=osc[k][:, grp, :], in_=gr[k, grp][:])

        def store_words(k, grp):
            tok = slice(k * 512, (k + 1) * 512)
            nc.sync.dma_start(
                out=out_1[grp, :, tok, :].rearrange("p m t -> p (m t)").bitcast(I32), in_=oc[k][:, grp, :].bitcast(I32)
            )

        def store_scales(k):
            tok = slice(k * 512, (k + 1) * 512)
            for Q in range(4):
                nc.sync.dma_start(
                    out=out_2[:, 4 * Q : 4 * Q + 4, tok].rearrange("g q m -> q g m").bitcast(I32),
                    in_=osc[k][32 * Q : 32 * Q + 4, :, :].bitcast(I32),
                )

        with tc.manual_schedule():
            z_turn(0, 0)
            z_turn(0, 1)
            load_z(1, 1, 1)
            load_rows(u_sb, u, "u", 0, 1)
            load_rows(v_sb, v, "v", 1, 0)
            k_make(0, 0)
            z_turn(0, 2)
            k_make(0, 1)
            k_make(0, 2)
            q_make(0, 0)
            z_turn(0, 3)
            q_make(0, 1)
            k_make(0, 3)
            q_make(0, 2)
            q_make(0, 3)
            interleave_q(0, 0, 0, "v")
            quant_k(0, 1)
            quant_q(0, 0)
            quant_k(0, 0)
            interleave_q(0, 1, 0, "v")
            quant_q(0, 1)
            v_turn(0, 0, 0)
            v_copy(0, 0, 0)
            v_turn(0, 0, 1)
            scores(0, 1, 3)
            relu_root(0, 1, 3, "s")
            scores(0, 1, 2)
            v_copy(0, 0, 1)
            v_turn(0, 1, 0)
            scores(0, 1, 1)
            relu_root(0, 1, 2, "s")
            scores(0, 1, 0)
            relu_root(0, 1, 1, "s")
            scores(0, 0, 3)
            v_copy(0, 1, 0)
            v_turn(0, 1, 1)
            relu_root(0, 1, 0, "s")
            scores(0, 0, 2)
            scores(0, 0, 1)
            relu_root(0, 0, 3, "s")
            scores(0, 0, 0)
            relu_root(0, 0, 2, "s")
            v_copy(0, 1, 1)
            v_turn(0, 0, 2)
            relu_root(0, 0, 1, "s")
            relu_root(0, 0, 0, "s")
            quant_v(0, 0, 0)
            v_copy(0, 0, 2)
            v_turn(0, 0, 3)
            load_rows(v_sb, v, "v", 1, 1)
            load_rows(u_sb, u, "u", 1, 0)
            quant_v(0, 1, 0)
            v_turn(0, 1, 2)
            v_copy(0, 0, 3)
            square(0, "s")
            v_turn(0, 1, 3)
            v_copy(0, 1, 2)
            quant_v(0, 0, 1)
            z_turn(1, 0)
            v_copy(0, 1, 3)
            quant_v(0, 1, 1)
            silu(0)
            zq_turn(1, 0, 0)
            scores(1, 0, 0)
            relu_root(1, 0, 0, "s")
            q_plane(1, 0, 0)
            scores(1, 0, 1)
            k_make(1, 0)
            zq_turn(1, 0, 1)
            relu_root(1, 0, 1, "s")
            q_plane(1, 0, 1)
            z_turn(1, 1)
            scores(1, 0, 2)
            square(1, "s")
            relu_root(1, 0, 2, "s")
            q_plane(1, 0, 2)
            quant_p(0)
            scores(1, 0, 3)
            zq_turn(1, 1, 0)
            relu_root(1, 0, 3, "s")
            q_plane(1, 0, 3)
            k_make(1, 1)
            interleave_q(1, 0, 0, "v")
            scores(1, 1, 0)
            st2(0, 0)
            st2(0, 1)
            quant_k(1, 0)
            relu_root(1, 1, 0, "s")
            z_turn(1, 2)
            q_plane(1, 1, 0)
            silu(1)
            load_rows(u_sb, u, "u", 1, 1)
            zq_turn(1, 1, 1)
            scores(1, 1, 1)
            relu_root(1, 1, 1, "s")
            q_plane(1, 1, 1)
            apply_gate(0, 0)
            apply_gate(0, 1)
            store_out(0)
            k_make(1, 2)
            scores(1, 1, 2)
            relu_root(1, 1, 2, "s")
            q_plane(1, 1, 2)
            st2(1, 0)
            st2(1, 1)
            scores(1, 1, 3)
            z_turn(1, 3)
            quant_q(1, 0)
            relu_root(1, 1, 3, "s")
            square(2, "s")
            q_plane(1, 1, 3)
            v_turn(1, 0, 0)
            scores(2, 0, 0)
            quant_p(1)
            k_make(1, 3)
            apply_gate(1, 0)
            apply_gate(1, 1)
            store_out(1)
            relu_root(2, 0, 0, "s")
            scores(2, 0, 1)
            interleave_q(1, 1, 0, "v")
            st2(2, 0)
            st2(2, 1)
            relu_root(2, 0, 1, "s")
            v_turn(1, 0, 1)
            scores(2, 0, 2)
            silu(2)
            v_copy(1, 0, 0)
            quant_q(1, 1)
            quant_k(1, 1)
            relu_root(2, 0, 2, "s")
            scores(2, 0, 3)
            apply_gate(2, 0)
            apply_gate(2, 1)
            store_out(2)
            v_turn(1, 1, 0)
            relu_root(2, 0, 3, "s")
            v_copy(1, 0, 1)
            scores(2, 1, 0)
            st2(3, 0)
            st2(3, 1)
            relu_root(2, 1, 0, "s")
            square(3, "s")
            scores(2, 1, 1)
            v_turn(1, 1, 1)
            quant_p(2)
            v_copy(1, 1, 0)
            apply_gate(3, 0)
            relu_root(2, 1, 1, "s")
            apply_gate(3, 1)
            store_out(3)
            scores(2, 1, 2)
            quant_v(1, 0, 0)
            st2(4, 0)
            st2(4, 1)
            relu_root(2, 1, 2, "s")
            scores(2, 1, 3)
            v_turn(1, 0, 2)
            v_copy(1, 1, 1)
            round_out(0, 0, 1024, "v")
            silu(3)
            relu_root(2, 1, 3, "s")
            scores(3, 0, 0)
            apply_gate(4, 0)
            apply_gate(4, 1)
            store_out(4)
            relu_root(3, 0, 0, "s")
            scores(3, 0, 1)
            v_copy(1, 0, 2)
            v_turn(1, 0, 3)
            st2(5, 0)
            st2(5, 1)
            round_out(1, 0, 1024, "v")
            quant_v(1, 1, 0)
            scores(3, 0, 2)
            relu_root(3, 0, 1, "s")
            square(4, "s")
            v_copy(1, 0, 3)
            quant_p(3)
            scores(3, 0, 3)
            turn(1, 0)
            relu_root(3, 0, 2, "s")
            v_turn(1, 1, 2)
            turn_copy(1, 0)
            apply_gate(5, 0)
            apply_gate(5, 1)
            store_out(5)
            turn(1, 1)
            round_out(2, 0, 1024, "v")
            st2(6, 0)
            scores(3, 1, 0)
            st2(6, 1)
            relu_root(3, 0, 3, "s")
            v_copy(1, 1, 2)
            v_turn(1, 1, 3)
            scores(3, 1, 1)
            silu(4)
            quant_v(1, 0, 1)
            relu_root(3, 1, 0, "s")
            turn_copy(1, 1)
            apply_gate(6, 0)
            apply_gate(6, 1)
            store_out(6)
            round_out(3, 0, 1024, "v")
            scores(3, 1, 2)
            relu_root(3, 1, 1, "s")
            v_copy(1, 1, 3)
            st2(7, 0)
            st2(7, 1)
            scores(3, 1, 3)
            relu_root(3, 1, 2, "s")
            turn(3, 0)
            square(5, "s")
            turn_copy(3, 0)
            turn(3, 1)
            round_out(4, 0, 1024, "v")
            relu_root(3, 1, 3, "s")
            quant_p(4)
            quant_v(1, 1, 1)
            apply_gate(7, 0)
            apply_gate(7, 1)
            store_out(7)
            st2(8, 0)
            st2(8, 1)
            turn_copy(3, 1)
            round_out(5, 0, 1024, "v")
            silu(5)
            apply_gate(8, 0)
            apply_gate(8, 1)
            store_out(8)
            st2(9, 0)
            turn(5, 0)
            st2(9, 1)
            turn(5, 1)
            round_out(6, 0, 1024, "v")
            turn_copy(5, 0)
            square(6, "s")
            quant_p(5)
            apply_gate(9, 0)
            apply_gate(9, 1)
            store_out(9)
            quant_out(0, 0)
            store_words(0, 0)
            st2(10, 0)
            st2(10, 1)
            round_out(7, 0, 1024, "v")
            turn_copy(5, 1)
            silu(6)
            turn(7, 0)
            apply_gate(10, 0)
            apply_gate(10, 1)
            store_out(10)
            round_out(8, 0, 1024, "v")
            turn(7, 1)
            st2(11, 0)
            st2(11, 1)
            turn_copy(7, 0)
            square(7, "s")
            quant_out(0, 1)
            store_words(0, 1)
            store_scales(0)
            round_out(9, 0, 1024, "v")
            quant_p(6)
            apply_gate(11, 0)
            apply_gate(11, 1)
            store_out(11)
            turn_copy(7, 1)
            st2(12, 0)
            st2(12, 1)
            turn(9, 0)
            round_out(10, 0, 1024, "v")
            turn(9, 1)
            silu(7)
            apply_gate(12, 0)
            apply_gate(12, 1)
            store_out(12)
            quant_out(1, 0)
            store_words(1, 0)
            st2(13, 0)
            st2(13, 1)
            turn_copy(9, 0)
            round_out(11, 0, 1024, "v")
            apply_gate(13, 0)
            quant_p(7)
            apply_gate(13, 1)
            store_out(13)
            turn_copy(9, 1)
            st2(14, 0)
            st2(14, 1)
            turn(11, 0)
            round_out(12, 0, 1024, "v")
            turn(11, 1)
            quant_out(1, 1)
            store_words(1, 1)
            store_scales(1)
            apply_gate(14, 0)
            apply_gate(14, 1)
            store_out(14)
            turn_copy(11, 0)
            round_out(13, 0, 1024, "v")
            st2(15, 0)
            st2(15, 1)
            turn_copy(11, 1)
            turn(13, 0)
            round_out(14, 0, 1024, "v")
            apply_gate(15, 0)
            apply_gate(15, 1)
            store_out(15)
            turn(13, 1)
            quant_out(2, 0)
            store_words(2, 0)
            round_out(15, 0, 512, "v")
            turn_copy(13, 0)
            round_out(15, 512, 1024, "v")
            turn(15, 0)
            turn_copy(13, 1)
            turn(15, 1)
            quant_out(2, 1)
            store_words(2, 1)
            store_scales(2)
            turn_copy(15, 0)
            turn_copy(15, 1)
            quant_out(3, 0)
            store_words(3, 0)
            quant_out(3, 1)
            store_words(3, 1)
            store_scales(3)
